import numpy as np
import ml_dtypes


def mxq(x, axis, fmt="e4m3"):
    dtype, down = {"e4m3": (ml_dtypes.float8_e4m3fn, 7), "e5m2": (ml_dtypes.float8_e5m2, 14)}[fmt]
    v = np.moveaxis(np.asarray(x, np.float32).astype(ml_dtypes.bfloat16).astype(np.float64), axis, -1)
    blocks = v.reshape(v.shape[:-1] + (-1, 32))
    amax = np.abs(blocks).max(-1, keepdims=True)
    byte = np.maximum(np.where(amax > 0, np.frexp(amax)[1] - 1 + 127, 0) - down, 1)
    scale = np.exp2(byte - 127.0)
    codes = (blocks / scale).astype(np.float32).astype(dtype).astype(np.float64)
    return np.moveaxis((codes * scale).reshape(v.shape), -1, axis)


WIDE = False


def mx_kscale(k):
    if not WIDE:
        return np.ones(k)
    levels = np.array([10, -10, 5, -5, 0])
    if k % 512:
        return np.exp2(np.random.permutation(np.resize(levels, k // 32))).repeat(32)
    a = np.empty((k // 512, 16))
    for p in range(k // 512):
        a[p, :8] = np.random.permutation(np.resize(levels, 8))
        for g in range(8):
            far = levels[np.abs(levels - a[p, g]) >= 10]
            a[p, g + 8] = far[np.random.randint(len(far))]
    return np.exp2(a.ravel()).repeat(32)


def f64(x):
    return np.asarray(x).astype(np.float64)


def striped(idx):
    return np.tile(idx.reshape(-1, 16).T, (8, 1)).astype(np.uint16)


def unstriped(offs):
    return offs[:16].T.reshape(-1).astype(np.int64)


def striped8(idx):
    return np.concatenate([x.reshape(-1, 16).T for x in idx]).astype(np.uint16)


def runs(offs, k):
    lists = np.stack([offs[16 * r : 16 * r + 16].T.reshape(-1) for r in range(8)]).astype(np.int64)
    return lists[np.arange(k) % 512 // 64]


def pack_weight(w):
    k, n = w.shape
    w = f64(np.asarray(w, np.float32).astype(ml_dtypes.bfloat16)).reshape(k // 32, 32, n)
    amax = np.abs(w).max(1)
    byte = np.clip(np.where(amax > 0, np.frexp(amax)[1] - 1 + 127 - 7, 1), 1, 254)
    scaled = (w * np.exp2(127.0 - byte)[:, None, :]).reshape(k, n).astype(np.float32)
    words = np.ascontiguousarray(scaled.reshape(k // 512, 128, 4, n).transpose(0, 1, 3, 2)).astype(ml_dtypes.float8_e4m3fn).view(np.uint8)
    return words, np.ascontiguousarray(byte.astype(np.uint8).reshape(k // 512, 16, n))


def unpack_weight(words, scales):
    g, p, n, _ = words.shape
    vals = np.ascontiguousarray(words).view(ml_dtypes.float8_e4m3fn).astype(np.float64) * np.repeat(np.exp2(scales.astype(np.float64) - 127.0), 8, axis=1)[..., None]
    return vals.transpose(0, 1, 3, 2).reshape(g * 512, n)


def relu(v):
    return np.maximum(v, 0.0)


K, T, S, H, N, V = 512, 2048, 1024, 512, 256, 512


def setup_inputs():
    n = np.random.standard_normal
    s = mx_kscale(K)[:, None]
    u = mx_kscale(H)
    packed_xT = pack_weight(n((K, T)) * s)
    return {
        "x_words": packed_xT[0],
        "x_scales": packed_xT[1],
        "w1": (n((K, H)) / np.sqrt(K) / s * u).astype(np.float32),
        "w2": (n((H, N)) / np.sqrt(H) / u[:, None]).astype(np.float32),
        "offs": striped8(np.stack([np.random.permutation(T)[:S] for _ in range(8)])),
        "left": striped(np.random.permutation(S)[:V]),
        "right": striped(np.random.permutation(S)[:V]),
    }


def reference(x_words, x_scales, w1, w2, offs, left, right):
    xq = unpack_weight(x_words, x_scales)[np.arange(K)[:, None], runs(offs, K)]
    h = mxq(f64(w1), 0, "e4m3").T @ xq
    z = relu(h[:, unstriped(left)] - h[:, unstriped(right)])
    return mxq(f64(w2), 0, "e4m3").T @ mxq(z, 0, "e4m3")

@@ -1,0 +1,161 @@
+from contextlib import ExitStack
+
+import concourse.mybir as mybir
+
+K, T, S, H, N, V = 512, 2048, 1024, 512, 256, 512
+FLOPS = 2 * K * H * S + 2 * H * N * V
+
+F32 = mybir.dt.float32
+BF16 = mybir.dt.bfloat16
+I32 = mybir.dt.int32
+U32 = mybir.dt.uint32
+U16 = mybir.dt.uint16
+U8 = mybir.dt.uint8
+FP8X4 = mybir.dt.float8_e4m3fn_x4
+RELU = mybir.ActivationFunctionType.Relu
+SUBTRACT = mybir.AluOpType.subtract
+MAX = mybir.AluOpType.max
+
+P = 128
+PACK = 4
+LIST = 16
+BANK = 512
+FETCH_SLICES = ((0, 384), (384, 128))
+HALF = V // 2
+
+
+def tile_picked_phpair_relu_p_kernel(tc, x_words, x_scales, w1, w2, offs, left, right, out):
+    nc = tc.nc
+    with ExitStack() as ctx:
+        held = ctx.enter_context(tc.tile_pool(name="held", bufs=1))
+        ring = ctx.enter_context(tc.tile_pool(name="ring", bufs=3))
+        h_psum = ctx.enter_context(tc.psum_pool(name="h_psum", bufs=4))
+        out_psum = ctx.enter_context(tc.psum_pool(name="out_psum", bufs=1))
+
+        offs_sb = held.tile([P, S // LIST], U16, name="offs_sb")
+        left_sb = held.tile([P, V // LIST], U16, name="left_sb")
+        right_sb = held.tile([P, V // LIST], U16, name="right_sb")
+        scale_table = held.tile([P, T], U8, name="scale_table", align_bytes=64)
+        word_table = held.tile([P, T], U32, name="word_table", align_bytes=64)
+        w1_raw = [held.tile([P, PACK, H // 2], F32, name="w1_raw%d" % c, align_bytes=64) for c in range(2)]
+        w2_raw = held.tile([P, PACK, N], F32, name="w2_raw", align_bytes=64)
+
+        nc.sync.dma_start(offs_sb[:], offs)
+        scale_rows = x_scales[0].bitcast(I32)
+        nc.sync.dma_start(scale_table[:].bitcast(I32), scale_rows.unsqueeze(1).to_broadcast([16, 8, T // 4]))
+        nc.sync.dma_start(word_table[:].bitcast(I32), x_words[0].rearrange("p n t -> p (n t)").bitcast(I32))
+        nc.sync.dma_start(right_sb[:], right)
+        nc.sync.dma_start(left_sb[:], left)
+        w1_rows = w1.rearrange("(p j) c -> p j c", j=PACK)
+        for c in range(2):
+            nc.sync.dma_start(w1_raw[c][:], w1_rows[:, :, c * (H // 2) : (c + 1) * (H // 2)])
+        nc.sync.dma_start(w2_raw[:], w2.rearrange("(p j) n -> p j n", j=PACK))
+
+        x_plane = held.tile([P, S], U8, name="x_plane", align_bytes=64)
+        nc.vector.memset(x_plane[:].bitcast(I32), 0)
+        picked_scales = held.tile([P, S], U8, name="picked_scales", align_bytes=64)
+        nc.vector.tensor_copy(picked_scales[:], scale_table[:].indirect(offs_sb[:]))
+        for i in range(4):
+            nc.scalar.dma_start(x_plane[i:P:32, :].bitcast(I32), picked_scales[8 * i : P : 32, :].bitcast(I32))
+
+        x_codes = []
+        for half in range(S // BANK):
+            codes = held.tile([P, BANK], U32, name="x_codes%d" % half, align_bytes=64)
+            cols = slice(half * BANK // LIST, (half + 1) * BANK // LIST)
+            nc.vector.tensor_copy(codes[:], word_table[:].indirect(offs_sb[:, cols]))
+            x_codes.append(codes)
+
+        w1_bf = held.tile([P, PACK, P, PACK], BF16, name="w1_bf", align_bytes=64)
+        for c, m0, m1, copy in ((0, 0, 64, nc.scalar.copy), (1, 0, 32, nc.scalar.copy), (1, 32, 64, nc.vector.tensor_copy)):
+            copy(
+                w1_bf[:, :, 64 * c + m0 : 64 * c + m1, :].rearrange("p t m j -> p m j t"),
+                w1_raw[c][:, :, PACK * m0 : PACK * m1].rearrange("p j (m t) -> p m j t", t=PACK),
+            )
+        w1_codes = held.tile([P, H], U32, name="w1_codes", align_bytes=64)
+        w1_scales = held.tile([P, H], U8, name="w1_scales", align_bytes=64)
+        for t0, t1 in ((0, 1), (1, 2), (2, 4)):
+            nc.vector.quantize_mx(
+                out=w1_codes[:, t0 * P : t1 * P].bitcast(FP8X4),
+                scales=w1_scales[:, t0 * P : t1 * P],
+                in_=w1_bf[:, t0:t1, :, :].rearrange("p t m j -> p (t m j)"),
+            )
+
+        w2_bf = held.tile([P, N, PACK], BF16, name="w2_bf", align_bytes=64)
+        nc.vector.tensor_copy(
+            w2_bf[:].rearrange("p (c i) j -> p c j i", i=4),
+            w2_raw[:].rearrange("p j (c i) -> p c j i", i=4),
+        )
+        w2_codes = held.tile([P, N], U32, name="w2_codes", align_bytes=64)
+        w2_scales = held.tile([P, N], U8, name="w2_scales", align_bytes=64)
+        nc.vector.quantize_mx(out=w2_codes[:].bitcast(FP8X4), scales=w2_scales[:], in_=w2_bf[:].rearrange("p n j -> p (n j)"))
+
+        h = []
+        for t in range(PACK):
+            h_t = held.tile([P, S], F32, name="h%d" % t, align_bytes=64)
+            for half in range(S // BANK):
+                cols = slice(half * BANK, (half + 1) * BANK)
+                bank = h_psum.tile([P, BANK], F32, name="h_bank")
+                nc.tensor.matmul_mx(
+                    out=bank[:],
+                    lhsT=w1_codes[:, t * P : (t + 1) * P].bitcast(FP8X4),
+                    lhsT_scale=w1_scales[:, t * P : (t + 1) * P],
+                    rhs=x_codes[half][:].bitcast(FP8X4),
+                    rhs_scale=x_plane[:, cols],
+                    start=True,
+                    stop=True,
+                )
+                nc.scalar.copy(h_t[:, cols], bank[:])
+            h.append(h_t)
+
+        diffs = [held.tile([P, PACK, w], F32, name="diff%d" % s, align_bytes=64) for s, (v0, w) in enumerate(FETCH_SLICES)]
+
+        def list_cols(s):
+            v0, w = FETCH_SLICES[s]
+            return slice(v0 // LIST, (v0 + w) // LIST)
+
+        def fetch_right(s, t):
+            fetched = ring.tile([P, FETCH_SLICES[s][1]], F32, name="fetched", align_bytes=64)
+            nc.vector.tensor_copy(fetched[:], h[t][:].indirect(right_sb[:, list_cols(s)]))
+            return fetched
+
+        def subtract(s, t, fetched):
+            nc.vector.tensor_tensor(diffs[s][:, t, :], h[t][:].indirect(left_sb[:, list_cols(s)]), fetched[:], SUBTRACT)
+
+        steps = [(s, t) for s in range(len(FETCH_SLICES)) for t in range(PACK)]
+        pending = fetch_right(*steps[0])
+        for n, (s, t) in enumerate(steps):
+            ahead = fetch_right(*steps[n + 1]) if n + 1 < len(steps) else None
+            subtract(s, t, pending)
+            pending = ahead
+
+        def woven(z_cols):
+            return z_cols.rearrange("p (c i) t -> p c t i", i=4)
+
+        def planes(diff_cols):
+            return diff_cols.rearrange("p t (c i) -> p c t i", i=4)
+
+        z_bf = [held.tile([P, HALF, PACK], BF16, name="z_bf%d" % half, align_bytes=64) for half in range(2)]
+        nc.scalar.activation(woven(z_bf[0][:]), planes(diffs[0][:, :, 0:HALF]), RELU)
+        nc.scalar.activation(woven(z_bf[1][:, 0:128, :]), planes(diffs[0][:, :, HALF:384]), RELU)
+        nc.vector.tensor_scalar(woven(z_bf[1][:, 128:HALF, :]), planes(diffs[1][:]), 0.0, None, MAX)
+
+        out_rows = out.rearrange("(a p) v -> p a v", p=P)
+        for half in range(2):
+            z_codes = held.tile([P, HALF], U32, name="z_codes%d" % half, align_bytes=64)
+            z_scales = held.tile([P, HALF], U8, name="z_scales%d" % half, align_bytes=64)
+            nc.vector.quantize_mx(out=z_codes[:].bitcast(FP8X4), scales=z_scales[:], in_=z_bf[half][:].rearrange("p v t -> p (v t)"))
+            result = held.tile([P, N // P, HALF], F32, name="result%d" % half, align_bytes=64)
+            for a in range(N // P):
+                bank = out_psum.tile([P, HALF], F32, name="out_bank%d_%d" % (half, a))
+                nc.tensor.matmul_mx(
+                    out=bank[:],
+                    lhsT=w2_codes[:, a * P : (a + 1) * P].bitcast(FP8X4),
+                    lhsT_scale=w2_scales[:, a * P : (a + 1) * P],
+                    rhs=z_codes[:].bitcast(FP8X4),
+                    rhs_scale=z_scales[:],
+                    start=True,
+                    stop=True,
+                )
+                copy = nc.vector.tensor_copy if (half, a) == (1, 1) else nc.scalar.copy
+                copy(result[:, a, :], bank[:])
+            nc.sync.dma_start(out_rows[:, :, half * HALF : (half + 1) * HALF], result[:])

@@ -28,17 +28,14 @@ def tile_picked_phpair_relu_p_kernel(tc, x_words, x_scales, w1, w2, offs, left, 
     nc = tc.nc
     with ExitStack() as ctx:
         held = ctx.enter_context(tc.tile_pool(name="held", bufs=1))
-        ring = ctx.enter_context(tc.tile_pool(name="ring", bufs=3))
-        h_psum = ctx.enter_context(tc.psum_pool(name="h_psum", bufs=4))
-        out_psum = ctx.enter_context(tc.psum_pool(name="out_psum", bufs=1))
+        psum = ctx.enter_context(tc.psum_pool(name="psum", bufs=8))
 
         offs_sb = held.tile([P, S // LIST], U16, name="offs_sb")
         left_sb = held.tile([P, V // LIST], U16, name="left_sb")
         right_sb = held.tile([P, V // LIST], U16, name="right_sb")
-        scale_table = held.tile([P, T], U8, name="scale_table", align_bytes=64)
+        scale_table = held.tile([P, T], U8, name="scale_table", tag="scale_table_then_w2", align_bytes=64)
         word_table = held.tile([P, T], U32, name="word_table", align_bytes=64)
         w1_raw = [held.tile([P, PACK, H // 2], F32, name="w1_raw%d" % c, align_bytes=64) for c in range(2)]
-        w2_raw = held.tile([P, PACK, N], F32, name="w2_raw", align_bytes=64)
 
         nc.sync.dma_start(offs_sb[:], offs)
         scale_rows = x_scales[0].bitcast(I32)
@@ -49,14 +46,15 @@ def tile_picked_phpair_relu_p_kernel(tc, x_words, x_scales, w1, w2, offs, left, 
         w1_rows = w1.rearrange("(p j) c -> p j c", j=PACK)
         for c in range(2):
             nc.sync.dma_start(w1_raw[c][:], w1_rows[:, :, c * (H // 2) : (c + 1) * (H // 2)])
-        nc.sync.dma_start(w2_raw[:], w2.rearrange("(p j) n -> p j n", j=PACK))
 
         x_plane = held.tile([P, S], U8, name="x_plane", align_bytes=64)
         nc.vector.memset(x_plane[:].bitcast(I32), 0)
         picked_scales = held.tile([P, S], U8, name="picked_scales", align_bytes=64)
         nc.vector.tensor_copy(picked_scales[:], scale_table[:].indirect(offs_sb[:]))
         for i in range(4):
-            nc.scalar.dma_start(x_plane[i:P:32, :].bitcast(I32), picked_scales[8 * i : P : 32, :].bitcast(I32))
+            nc.sync.dma_start(x_plane[i:P:32, :].bitcast(I32), picked_scales[8 * i : P : 32, :].bitcast(I32))
+        w2_raw = held.tile([P, PACK, N], F32, name="w2_raw", tag="scale_table_then_w2", align_bytes=64)
+        nc.sync.dma_start(w2_raw[:], w2.rearrange("(p j) n -> p j n", j=PACK))
 
         x_codes = []
         for half in range(S // BANK):
@@ -65,8 +63,8 @@ def tile_picked_phpair_relu_p_kernel(tc, x_words, x_scales, w1, w2, offs, left, 
             nc.vector.tensor_copy(codes[:], word_table[:].indirect(offs_sb[:, cols]))
             x_codes.append(codes)
 
-        w1_bf = held.tile([P, PACK, P, PACK], BF16, name="w1_bf", align_bytes=64)
-        for c, m0, m1, copy in ((0, 0, 64, nc.scalar.copy), (1, 0, 32, nc.scalar.copy), (1, 32, 64, nc.vector.tensor_copy)):
+        w1_bf = held.tile([P, PACK, P, PACK], BF16, name="w1_bf", tag="weights_bf", align_bytes=64)
+        for c, m0, m1, copy in ((0, 0, 64, nc.scalar.copy), (1, 0, 24, nc.scalar.copy), (1, 24, 64, nc.vector.tensor_copy)):
             copy(
                 w1_bf[:, :, 64 * c + m0 : 64 * c + m1, :].rearrange("p t m j -> p m j t"),
                 w1_raw[c][:, :, PACK * m0 : PACK * m1].rearrange("p j (m t) -> p m j t", t=PACK),
@@ -80,7 +78,7 @@ def tile_picked_phpair_relu_p_kernel(tc, x_words, x_scales, w1, w2, offs, left, 
                 in_=w1_bf[:, t0:t1, :, :].rearrange("p t m j -> p (t m j)"),
             )
 
-        w2_bf = held.tile([P, N, PACK], BF16, name="w2_bf", align_bytes=64)
+        w2_bf = held.tile([P, N, PACK], BF16, name="w2_bf", tag="weights_bf", align_bytes=64)
         nc.vector.tensor_copy(
             w2_bf[:].rearrange("p (c i) j -> p c j i", i=4),
             w2_raw[:].rearrange("p j (c i) -> p c j i", i=4),
@@ -92,41 +90,28 @@ def tile_picked_phpair_relu_p_kernel(tc, x_words, x_scales, w1, w2, offs, left, 
         h = []
         for t in range(PACK):
             h_t = held.tile([P, S], F32, name="h%d" % t, align_bytes=64)
-            for half in range(S // BANK):
-                cols = slice(half * BANK, (half + 1) * BANK)
-                bank = h_psum.tile([P, BANK], F32, name="h_bank")
+            w = BANK // 2 if t == 0 else BANK
+            for c0 in range(0, S, w):
+                bank = psum.tile([P, w], F32, name="bank")
                 nc.tensor.matmul_mx(
                     out=bank[:],
                     lhsT=w1_codes[:, t * P : (t + 1) * P].bitcast(FP8X4),
                     lhsT_scale=w1_scales[:, t * P : (t + 1) * P],
-                    rhs=x_codes[half][:].bitcast(FP8X4),
-                    rhs_scale=x_plane[:, cols],
+                    rhs=x_codes[c0 // BANK][:, c0 % BANK : c0 % BANK + w].bitcast(FP8X4),
+                    rhs_scale=x_plane[:, c0 : c0 + w],
                     start=True,
                     stop=True,
                 )
-                nc.scalar.copy(h_t[:, cols], bank[:])
+                nc.scalar.copy(h_t[:, c0 : c0 + w], bank[:])
             h.append(h_t)
 
-        diffs = [held.tile([P, PACK, w], F32, name="diff%d" % s, align_bytes=64) for s, (v0, w) in enumerate(FETCH_SLICES)]
+        def fetch_right(fetched, t, v0):
+            w = fetched.shape[1]
+            nc.vector.tensor_copy(fetched, h[t][:].indirect(right_sb[:, v0 // LIST : (v0 + w) // LIST]))
 
-        def list_cols(s):
-            v0, w = FETCH_SLICES[s]
-            return slice(v0 // LIST, (v0 + w) // LIST)
-
-        def fetch_right(s, t):
-            fetched = ring.tile([P, FETCH_SLICES[s][1]], F32, name="fetched", align_bytes=64)
-            nc.vector.tensor_copy(fetched[:], h[t][:].indirect(right_sb[:, list_cols(s)]))
-            return fetched
-
-        def subtract(s, t, fetched):
-            nc.vector.tensor_tensor(diffs[s][:, t, :], h[t][:].indirect(left_sb[:, list_cols(s)]), fetched[:], SUBTRACT)
-
-        steps = [(s, t) for s in range(len(FETCH_SLICES)) for t in range(PACK)]
-        pending = fetch_right(*steps[0])
-        for n, (s, t) in enumerate(steps):
-            ahead = fetch_right(*steps[n + 1]) if n + 1 < len(steps) else None
-            subtract(s, t, pending)
-            pending = ahead
+        def subtract(diff, t, v0, fetched):
+            w = fetched.shape[1]
+            nc.vector.tensor_tensor(diff[:, t, :], h[t][:].indirect(left_sb[:, v0 // LIST : (v0 + w) // LIST]), fetched, SUBTRACT)
 
         def woven(z_cols):
             return z_cols.rearrange("p (c i) t -> p c t i", i=4)
@@ -134,19 +119,16 @@ def tile_picked_phpair_relu_p_kernel(tc, x_words, x_scales, w1, w2, offs, left, 
         def planes(diff_cols):
             return diff_cols.rearrange("p t (c i) -> p c t i", i=4)
 
-        z_bf = [held.tile([P, HALF, PACK], BF16, name="z_bf%d" % half, align_bytes=64) for half in range(2)]
-        nc.scalar.activation(woven(z_bf[0][:]), planes(diffs[0][:, :, 0:HALF]), RELU)
-        nc.scalar.activation(woven(z_bf[1][:, 0:128, :]), planes(diffs[0][:, :, HALF:384]), RELU)
-        nc.vector.tensor_scalar(woven(z_bf[1][:, 128:HALF, :]), planes(diffs[1][:]), 0.0, None, MAX)
-
         out_rows = out.rearrange("(a p) v -> p a v", p=P)
-        for half in range(2):
-            z_codes = held.tile([P, HALF], U32, name="z_codes%d" % half, align_bytes=64)
-            z_scales = held.tile([P, HALF], U8, name="z_scales%d" % half, align_bytes=64)
-            nc.vector.quantize_mx(out=z_codes[:].bitcast(FP8X4), scales=z_scales[:], in_=z_bf[half][:].rearrange("p v t -> p (v t)"))
-            result = held.tile([P, N // P, HALF], F32, name="result%d" % half, align_bytes=64)
-            for a in range(N // P):
-                bank = out_psum.tile([P, HALF], F32, name="out_bank%d_%d" % (half, a))
+
+        def second_product(z_bf, v0, copies):
+            w = z_bf.shape[1]
+            z_codes = held.tile([P, w], U32, name="z_codes%d" % v0, align_bytes=64)
+            z_scales = held.tile([P, w], U8, name="z_scales%d" % v0, align_bytes=64)
+            nc.vector.quantize_mx(out=z_codes[:].bitcast(FP8X4), scales=z_scales[:], in_=z_bf[:].rearrange("p v t -> p (v t)"))
+            result = held.tile([P, N // P, w], F32, name="result%d" % v0, align_bytes=64)
+            for a, copy in enumerate(copies):
+                bank = psum.tile([P, w], F32, name="bank")
                 nc.tensor.matmul_mx(
                     out=bank[:],
                     lhsT=w2_codes[:, a * P : (a + 1) * P].bitcast(FP8X4),
@@ -156,6 +138,26 @@ def tile_picked_phpair_relu_p_kernel(tc, x_words, x_scales, w1, w2, offs, left, 
                     start=True,
                     stop=True,
                 )
-                copy = nc.vector.tensor_copy if (half, a) == (1, 1) else nc.scalar.copy
                 copy(result[:, a, :], bank[:])
-            nc.sync.dma_start(out_rows[:, :, half * HALF : (half + 1) * HALF], result[:])
+            nc.sync.dma_start(out_rows[:, :, v0 : v0 + w], result[:])
+
+        WA, WB = 384, 128
+        diff_a = held.tile([P, PACK, WA], F32, name="diff_a", align_bytes=64)
+        fetched_b = held.tile([P, PACK, WB], F32, name="fetched_b", align_bytes=64)
+        for t in range(PACK):
+            fetched_a = held.tile([P, WA], F32, name="fetched_a", tag="fetched_a%d" % t, align_bytes=64)
+            fetch_right(fetched_a[:], t, 0)
+            fetch_right(fetched_b[:, t, :], t, WA)
+            subtract(diff_a, t, 0, fetched_a[:])
+
+        z_bf = [held.tile([P, HALF, PACK], BF16, name="z_bf%d" % half, align_bytes=64) for half in range(2)]
+        nc.scalar.activation(woven(z_bf[0][:]), planes(diff_a[:, :, 0:HALF]), RELU)
+        nc.scalar.activation(woven(z_bf[1][:, 0 : WA - HALF, :]), planes(diff_a[:, :, HALF:WA]), RELU)
+
+        diff_b = held.tile([P, PACK, WB], F32, name="diff_b", tag="fetched_a3", align_bytes=64)
+        for t in range(PACK):
+            subtract(diff_b, t, WA, fetched_b[:, t, :])
+
+        second_product(z_bf[0], 0, (nc.scalar.copy, nc.scalar.copy))
+        nc.vector.tensor_scalar(woven(z_bf[1][:, WA - HALF : HALF, :]), planes(diff_b[:]), 0.0, None, MAX)
+        second_product(z_bf[1], HALF, (nc.scalar.copy, nc.vector.tensor_copy))

@@ -37,9 +37,9 @@ def tile_picked_phpair_relu_p_kernel(tc, x_words, x_scales, w1, w2, offs, left, 
         word_table = held.tile([P, T], U32, name="word_table", align_bytes=64)
         w1_raw = [held.tile([P, PACK, H // 2], F32, name="w1_raw%d" % c, align_bytes=64) for c in range(2)]
 
-        nc.sync.dma_start(offs_sb[:], offs)
         scale_rows = x_scales[0].bitcast(I32)
         nc.sync.dma_start(scale_table[:].bitcast(I32), scale_rows.unsqueeze(1).to_broadcast([16, 8, T // 4]))
+        nc.sync.dma_start(offs_sb[:], offs)
         nc.sync.dma_start(word_table[:].bitcast(I32), x_words[0].rearrange("p n t -> p (n t)").bitcast(I32))
         nc.sync.dma_start(right_sb[:], right)
         nc.sync.dma_start(left_sb[:], left)
@@ -63,8 +63,8 @@ def tile_picked_phpair_relu_p_kernel(tc, x_words, x_scales, w1, w2, offs, left, 
             nc.vector.tensor_copy(codes[:], word_table[:].indirect(offs_sb[:, cols]))
             x_codes.append(codes)
 
-        w1_bf = held.tile([P, PACK, P, PACK], BF16, name="w1_bf", tag="weights_bf", align_bytes=64)
-        for c, m0, m1, copy in ((0, 0, 64, nc.scalar.copy), (1, 0, 24, nc.scalar.copy), (1, 24, 64, nc.vector.tensor_copy)):
+        w1_bf = held.tile([P, PACK, P, PACK], BF16, name="w1_bf", align_bytes=64)
+        for c, m0, m1, copy in ((0, 0, 64, nc.scalar.copy), (1, 0, 32, nc.scalar.copy), (1, 32, 64, nc.vector.tensor_copy)):
             copy(
                 w1_bf[:, :, 64 * c + m0 : 64 * c + m1, :].rearrange("p t m j -> p m j t"),
                 w1_raw[c][:, :, PACK * m0 : PACK * m1].rearrange("p j (m t) -> p m j t", t=PACK),
@@ -78,14 +78,18 @@ def tile_picked_phpair_relu_p_kernel(tc, x_words, x_scales, w1, w2, offs, left, 
                 in_=w1_bf[:, t0:t1, :, :].rearrange("p t m j -> p (t m j)"),
             )
 
-        w2_bf = held.tile([P, N, PACK], BF16, name="w2_bf", tag="weights_bf", align_bytes=64)
-        nc.vector.tensor_copy(
-            w2_bf[:].rearrange("p (c i) j -> p c j i", i=4),
-            w2_raw[:].rearrange("p j (c i) -> p c j i", i=4),
-        )
+        w2_bf = held.tile([P, N, PACK], BF16, name="w2_bf", align_bytes=64)
         w2_codes = held.tile([P, N], U32, name="w2_codes", align_bytes=64)
         w2_scales = held.tile([P, N], U8, name="w2_scales", align_bytes=64)
-        nc.vector.quantize_mx(out=w2_codes[:].bitcast(FP8X4), scales=w2_scales[:], in_=w2_bf[:].rearrange("p n j -> p (n j)"))
+        for a in range(N // P):
+            cols = slice(a * P, (a + 1) * P)
+            nc.vector.tensor_copy(
+                w2_bf[:, cols, :].rearrange("p (c i) j -> p c j i", i=4),
+                w2_raw[:, :, cols].rearrange("p j (c i) -> p c j i", i=4),
+            )
+        for a in range(N // P):
+            cols = slice(a * P, (a + 1) * P)
+            nc.vector.quantize_mx(out=w2_codes[:, cols].bitcast(FP8X4), scales=w2_scales[:, cols], in_=w2_bf[:, cols, :].rearrange("p n j -> p (n j)"))
 
         h = []
         for t in range(PACK):
@@ -111,7 +115,7 @@ def tile_picked_phpair_relu_p_kernel(tc, x_words, x_scales, w1, w2, offs, left, 
 
         def subtract(diff, t, v0, fetched):
             w = fetched.shape[1]
-            nc.vector.tensor_tensor(diff[:, t, :], h[t][:].indirect(left_sb[:, v0 // LIST : (v0 + w) // LIST]), fetched, SUBTRACT)
+            nc.vector.tensor_tensor(diff, h[t][:].indirect(left_sb[:, v0 // LIST : (v0 + w) // LIST]), fetched, SUBTRACT)
 
         def woven(z_cols):
             return z_cols.rearrange("p (c i) t -> p c t i", i=4)
@@ -121,11 +125,15 @@ def tile_picked_phpair_relu_p_kernel(tc, x_words, x_scales, w1, w2, offs, left, 
 
         out_rows = out.rearrange("(a p) v -> p a v", p=P)
 
-        def second_product(z_bf, v0, copies):
-            w = z_bf.shape[1]
+        def second_product(z_parts, v0, copies, stores):
+            w = HALF
             z_codes = held.tile([P, w], U32, name="z_codes%d" % v0, align_bytes=64)
             z_scales = held.tile([P, w], U8, name="z_scales%d" % v0, align_bytes=64)
-            nc.vector.quantize_mx(out=z_codes[:].bitcast(FP8X4), scales=z_scales[:], in_=z_bf[:].rearrange("p v t -> p (v t)"))
+            c0 = 0
+            for z_bf in z_parts:
+                cols = slice(c0, c0 + z_bf.shape[1])
+                nc.vector.quantize_mx(out=z_codes[:, cols].bitcast(FP8X4), scales=z_scales[:, cols], in_=z_bf[:].rearrange("p v t -> p (v t)"))
+                c0 = cols.stop
             result = held.tile([P, N // P, w], F32, name="result%d" % v0, align_bytes=64)
             for a, copy in enumerate(copies):
                 bank = psum.tile([P, w], F32, name="bank")
@@ -139,25 +147,37 @@ def tile_picked_phpair_relu_p_kernel(tc, x_words, x_scales, w1, w2, offs, left, 
                     stop=True,
                 )
                 copy(result[:, a, :], bank[:])
-            nc.sync.dma_start(out_rows[:, :, v0 : v0 + w], result[:])
+            for store, a0, a1 in stores:
+                store(out_rows[:, a0:a1, v0 : v0 + w], result[:, a0:a1, :])
 
         WA, WB = 384, 128
         diff_a = held.tile([P, PACK, WA], F32, name="diff_a", align_bytes=64)
-        fetched_b = held.tile([P, PACK, WB], F32, name="fetched_b", align_bytes=64)
+        late = []
+        for t in range(PACK - 1):
+            fetched = held.tile([P, V], F32, name="fetched%d" % t, align_bytes=64)
+            fetch_right(fetched[:, 0:WA], t, 0)
+            fetch_right(fetched[:, WA:V], t, WA)
+            subtract(diff_a[:, t, :], t, 0, fetched[:, 0:WA])
+            late.append(fetched[:, WA:V])
+        t = PACK - 1
+        first_half = held.tile([P, HALF], F32, name="first_half", tag="first_half_then_diff_b", align_bytes=64)
+        second_half = held.tile([P, HALF], F32, name="second_half", align_bytes=64)
+        fetch_right(first_half[:], t, 0)
+        fetch_right(second_half[:], t, HALF)
+        subtract(diff_a[:, t, 0:HALF], t, 0, first_half[:])
+        subtract(diff_a[:, t, HALF:WA], t, HALF, second_half[:, 0 : WA - HALF])
+        late.append(second_half[:, WA - HALF : HALF])
+
+        z_a0 = held.tile([P, HALF, PACK], BF16, name="z_a0", tag="z_first_last", align_bytes=64)
+        z_a1 = held.tile([P, WA - HALF, PACK], BF16, name="z_a1", align_bytes=64)
+        nc.scalar.activation(woven(z_a0[:]), planes(diff_a[:, :, 0:HALF]), RELU)
+        nc.scalar.activation(woven(z_a1[:]), planes(diff_a[:, :, HALF:WA]), RELU)
+
+        diff_b = held.tile([P, PACK, WB], F32, name="diff_b", tag="first_half_then_diff_b", align_bytes=64)
         for t in range(PACK):
-            fetched_a = held.tile([P, WA], F32, name="fetched_a", tag="fetched_a%d" % t, align_bytes=64)
-            fetch_right(fetched_a[:], t, 0)
-            fetch_right(fetched_b[:, t, :], t, WA)
-            subtract(diff_a, t, 0, fetched_a[:])
+            subtract(diff_b[:, t, :], t, WA, late[t])
 
-        z_bf = [held.tile([P, HALF, PACK], BF16, name="z_bf%d" % half, align_bytes=64) for half in range(2)]
-        nc.scalar.activation(woven(z_bf[0][:]), planes(diff_a[:, :, 0:HALF]), RELU)
-        nc.scalar.activation(woven(z_bf[1][:, 0 : WA - HALF, :]), planes(diff_a[:, :, HALF:WA]), RELU)
-
-        diff_b = held.tile([P, PACK, WB], F32, name="diff_b", tag="fetched_a3", align_bytes=64)
-        for t in range(PACK):
-            subtract(diff_b, t, WA, fetched_b[:, t, :])
-
-        second_product(z_bf[0], 0, (nc.scalar.copy, nc.scalar.copy))
-        nc.vector.tensor_scalar(woven(z_bf[1][:, WA - HALF : HALF, :]), planes(diff_b[:]), 0.0, None, MAX)
-        second_product(z_bf[1], HALF, (nc.scalar.copy, nc.vector.tensor_copy))
+        second_product((z_a0,), 0, (nc.scalar.copy, nc.scalar.copy), ((nc.sync.dma_start, 0, 2),))
+        z_b = held.tile([P, WB, PACK], BF16, name="z_b", tag="z_first_last", align_bytes=64)
+        nc.vector.tensor_scalar(woven(z_b[:]), planes(diff_b[:]), 0.0, None, MAX)
+        second_product((z_a1, z_b), HALF, (nc.scalar.copy, nc.vector.tensor_copy), ((nc.scalar.dma_start, 0, 1), (nc.sync.dma_start, 1, 2)))

@@ -19,9 +19,13 @@ MAX = mybir.AluOpType.max
 P = 128
 PACK = 4
 LIST = 16
+BLOCKS = K // 32
+BLOCK_PARTITIONS = P // BLOCKS
+QUADRANT = 32
 BANK = 512
-FETCH_SLICES = ((0, 384), (384, 128))
+RUN = 4
 HALF = V // 2
+EARLY = 3 * V // 4
 
 
 def tile_picked_phpair_relu_p_kernel(tc, x_words, x_scales, w1, w2, offs, left, right, out):
@@ -33,151 +37,150 @@ def tile_picked_phpair_relu_p_kernel(tc, x_words, x_scales, w1, w2, offs, left, 
         offs_sb = held.tile([P, S // LIST], U16, name="offs_sb")
         left_sb = held.tile([P, V // LIST], U16, name="left_sb")
         right_sb = held.tile([P, V // LIST], U16, name="right_sb")
-        scale_table = held.tile([P, T], U8, name="scale_table", tag="scale_table_then_w2", align_bytes=64)
+        scale_table = held.tile([P, T], U8, name="scale_table", align_bytes=64)
         word_table = held.tile([P, T], U32, name="word_table", align_bytes=64)
-        w1_raw = [held.tile([P, PACK, H // 2], F32, name="w1_raw%d" % c, align_bytes=64) for c in range(2)]
+        w1_raw = [held.tile([P, PACK, H // 2], F32, name="w1_raw", tag="weights_raw%d" % c, align_bytes=64) for c in range(2)]
 
-        scale_rows = x_scales[0].bitcast(I32)
-        nc.sync.dma_start(scale_table[:].bitcast(I32), scale_rows.unsqueeze(1).to_broadcast([16, 8, T // 4]))
+        scale_rows = x_scales[0].bitcast(I32).unsqueeze(1).to_broadcast([BLOCKS, BLOCK_PARTITIONS, T // 4])
+        nc.sync.dma_start(scale_table[:].bitcast(I32), scale_rows)
         nc.sync.dma_start(offs_sb[:], offs)
         nc.sync.dma_start(word_table[:].bitcast(I32), x_words[0].rearrange("p n t -> p (n t)").bitcast(I32))
-        nc.sync.dma_start(right_sb[:], right)
-        nc.sync.dma_start(left_sb[:], left)
         w1_rows = w1.rearrange("(p j) c -> p j c", j=PACK)
         for c in range(2):
             nc.sync.dma_start(w1_raw[c][:], w1_rows[:, :, c * (H // 2) : (c + 1) * (H // 2)])
+        nc.sync.dma_start(right_sb[:], right)
+        nc.sync.dma_start(left_sb[:], left)
 
-        x_plane = held.tile([P, S], U8, name="x_plane", align_bytes=64)
-        nc.vector.memset(x_plane[:].bitcast(I32), 0)
+        warm_in = held.tile([P, 1], F32, name="warm_in")
+        warm_out = held.tile([P, 1], F32, name="warm_out")
+        nc.vector.memset(warm_in[:], 0.0)
+        nc.scalar.activation(warm_out[:], warm_in[:], RELU)
+
+        x_scale_rows = held.tile([P, S], U8, name="x_scale_rows", align_bytes=64)
+        nc.vector.memset(x_scale_rows[:].bitcast(I32), 0)
         picked_scales = held.tile([P, S], U8, name="picked_scales", align_bytes=64)
         nc.vector.tensor_copy(picked_scales[:], scale_table[:].indirect(offs_sb[:]))
-        for i in range(4):
-            nc.sync.dma_start(x_plane[i:P:32, :].bitcast(I32), picked_scales[8 * i : P : 32, :].bitcast(I32))
-        w2_raw = held.tile([P, PACK, N], F32, name="w2_raw", tag="scale_table_then_w2", align_bytes=64)
-        nc.sync.dma_start(w2_raw[:], w2.rearrange("(p j) n -> p j n", j=PACK))
+        for i in range(QUADRANT // BLOCK_PARTITIONS):
+            nc.scalar.dma_start(
+                x_scale_rows[i:P:QUADRANT, :].bitcast(I32),
+                picked_scales[BLOCK_PARTITIONS * i : P : QUADRANT, :].bitcast(I32),
+            )
 
-        x_codes = []
-        for half in range(S // BANK):
-            codes = held.tile([P, BANK], U32, name="x_codes%d" % half, align_bytes=64)
-            cols = slice(half * BANK // LIST, (half + 1) * BANK // LIST)
-            nc.vector.tensor_copy(codes[:], word_table[:].indirect(offs_sb[:, cols]))
-            x_codes.append(codes)
+        x_codes = held.tile([P, S], U32, name="x_codes", tag="x_codes_then_w2_bf", align_bytes=64)
+        nc.vector.tensor_copy(x_codes[:], word_table[:].indirect(offs_sb[:]))
 
         w1_bf = held.tile([P, PACK, P, PACK], BF16, name="w1_bf", align_bytes=64)
-        for c, m0, m1, copy in ((0, 0, 64, nc.scalar.copy), (1, 0, 32, nc.scalar.copy), (1, 32, 64, nc.vector.tensor_copy)):
+        m_half = P // 2
+        shares = ((0, 0, m_half, nc.scalar.copy), (1, 0, m_half // 2, nc.scalar.copy), (1, m_half // 2, m_half, nc.vector.tensor_copy))
+        for c, m0, m1, copy in shares:
             copy(
-                w1_bf[:, :, 64 * c + m0 : 64 * c + m1, :].rearrange("p t m j -> p m j t"),
+                w1_bf[:, :, m_half * c + m0 : m_half * c + m1, :].rearrange("p t m j -> p m j t"),
                 w1_raw[c][:, :, PACK * m0 : PACK * m1].rearrange("p j (m t) -> p m j t", t=PACK),
             )
+        w2_raw = held.tile([P, PACK, N], F32, name="w2_raw", tag="weights_raw0", align_bytes=64)
+        nc.sync.dma_start(w2_raw[:], w2.rearrange("(p j) n -> p j n", j=PACK))
+
         w1_codes = held.tile([P, H], U32, name="w1_codes", align_bytes=64)
         w1_scales = held.tile([P, H], U8, name="w1_scales", align_bytes=64)
-        for t0, t1 in ((0, 1), (1, 2), (2, 4)):
+        for t0, t1 in ((0, 1), (1, 2), (2, PACK)):
             nc.vector.quantize_mx(
                 out=w1_codes[:, t0 * P : t1 * P].bitcast(FP8X4),
                 scales=w1_scales[:, t0 * P : t1 * P],
                 in_=w1_bf[:, t0:t1, :, :].rearrange("p t m j -> p (t m j)"),
             )
 
-        w2_bf = held.tile([P, N, PACK], BF16, name="w2_bf", align_bytes=64)
-        w2_codes = held.tile([P, N], U32, name="w2_codes", align_bytes=64)
-        w2_scales = held.tile([P, N], U8, name="w2_scales", align_bytes=64)
-        for a in range(N // P):
-            cols = slice(a * P, (a + 1) * P)
-            nc.vector.tensor_copy(
-                w2_bf[:, cols, :].rearrange("p (c i) j -> p c j i", i=4),
-                w2_raw[:, :, cols].rearrange("p j (c i) -> p c j i", i=4),
-            )
-        for a in range(N // P):
-            cols = slice(a * P, (a + 1) * P)
-            nc.vector.quantize_mx(out=w2_codes[:, cols].bitcast(FP8X4), scales=w2_scales[:, cols], in_=w2_bf[:, cols, :].rearrange("p n j -> p (n j)"))
+        def woven(values):
+            return values.rearrange("p (c r) t -> p c t r", r=RUN)
+
+        def by_slot(values):
+            return values.rearrange("p t (c r) -> p c t r", r=RUN)
 
         h = []
         for t in range(PACK):
-            h_t = held.tile([P, S], F32, name="h%d" % t, align_bytes=64)
-            w = BANK // 2 if t == 0 else BANK
-            for c0 in range(0, S, w):
-                bank = psum.tile([P, w], F32, name="bank")
+            h_plane = held.tile([P, S], F32, name="h%d" % t, align_bytes=64)
+            width = BANK // 2 if t == 0 else BANK
+            for c0 in range(0, S, width):
+                cols = slice(c0, c0 + width)
+                bank = psum.tile([P, width], F32, name="bank")
                 nc.tensor.matmul_mx(
                     out=bank[:],
                     lhsT=w1_codes[:, t * P : (t + 1) * P].bitcast(FP8X4),
                     lhsT_scale=w1_scales[:, t * P : (t + 1) * P],
-                    rhs=x_codes[c0 // BANK][:, c0 % BANK : c0 % BANK + w].bitcast(FP8X4),
-                    rhs_scale=x_plane[:, c0 : c0 + w],
+                    rhs=x_codes[:, cols].bitcast(FP8X4),
+                    rhs_scale=x_scale_rows[:, cols],
                     start=True,
                     stop=True,
                 )
-                nc.scalar.copy(h_t[:, c0 : c0 + w], bank[:])
-            h.append(h_t)
+                nc.scalar.copy(h_plane[:, cols], bank[:])
+            h.append(h_plane)
+
+        w2_bf = held.tile([P, N, PACK], BF16, name="w2_bf", tag="x_codes_then_w2_bf", align_bytes=64)
+        w2_codes = held.tile([P, N], U32, name="w2_codes", align_bytes=64)
+        w2_scales = held.tile([P, N], U8, name="w2_scales", align_bytes=64)
+        row_tiles = [slice(a * P, (a + 1) * P) for a in range(N // P)]
+        nc.scalar.copy(woven(w2_bf[:]), by_slot(w2_raw[:]))
+        nc.vector.quantize_mx(out=w2_codes[:].bitcast(FP8X4), scales=w2_scales[:], in_=w2_bf[:].rearrange("p n j -> p (n j)"))
+
+        def entries(list_sb, v0, count):
+            return list_sb[:, v0 // LIST : (v0 + count) // LIST]
 
         def fetch_right(fetched, t, v0):
-            w = fetched.shape[1]
-            nc.vector.tensor_copy(fetched, h[t][:].indirect(right_sb[:, v0 // LIST : (v0 + w) // LIST]))
+            nc.vector.tensor_copy(fetched, h[t][:].indirect(entries(right_sb, v0, fetched.shape[1])))
 
         def subtract(diff, t, v0, fetched):
-            w = fetched.shape[1]
-            nc.vector.tensor_tensor(diff, h[t][:].indirect(left_sb[:, v0 // LIST : (v0 + w) // LIST]), fetched, SUBTRACT)
-
-        def woven(z_cols):
-            return z_cols.rearrange("p (c i) t -> p c t i", i=4)
-
-        def planes(diff_cols):
-            return diff_cols.rearrange("p t (c i) -> p c t i", i=4)
+            nc.vector.tensor_tensor(diff, h[t][:].indirect(entries(left_sb, v0, fetched.shape[1])), fetched, SUBTRACT)
 
         out_rows = out.rearrange("(a p) v -> p a v", p=P)
 
-        def second_product(z_parts, v0, copies, stores):
-            w = HALF
-            z_codes = held.tile([P, w], U32, name="z_codes%d" % v0, align_bytes=64)
-            z_scales = held.tile([P, w], U8, name="z_scales%d" % v0, align_bytes=64)
-            c0 = 0
-            for z_bf in z_parts:
-                cols = slice(c0, c0 + z_bf.shape[1])
-                nc.vector.quantize_mx(out=z_codes[:, cols].bitcast(FP8X4), scales=z_scales[:, cols], in_=z_bf[:].rearrange("p v t -> p (v t)"))
-                c0 = cols.stop
-            result = held.tile([P, N // P, w], F32, name="result%d" % v0, align_bytes=64)
+        def second_product(z_bf, v0, copies, stores):
+            width = z_bf.shape[1]
+            z_codes = held.tile([P, width], U32, name="z_codes%d" % v0, align_bytes=64)
+            z_scales = held.tile([P, width], U8, name="z_scales%d" % v0, align_bytes=64)
+            nc.vector.quantize_mx(out=z_codes[:].bitcast(FP8X4), scales=z_scales[:], in_=z_bf[:].rearrange("p v t -> p (v t)"))
+            result = held.tile([P, N // P, width], F32, name="result%d" % v0, align_bytes=64)
             for a, copy in enumerate(copies):
-                bank = psum.tile([P, w], F32, name="bank")
+                bank = psum.tile([P, width], F32, name="bank")
                 nc.tensor.matmul_mx(
                     out=bank[:],
-                    lhsT=w2_codes[:, a * P : (a + 1) * P].bitcast(FP8X4),
-                    lhsT_scale=w2_scales[:, a * P : (a + 1) * P],
+                    lhsT=w2_codes[:, row_tiles[a]].bitcast(FP8X4),
+                    lhsT_scale=w2_scales[:, row_tiles[a]],
                     rhs=z_codes[:].bitcast(FP8X4),
                     rhs_scale=z_scales[:],
                     start=True,
                     stop=True,
                 )
                 copy(result[:, a, :], bank[:])
-            for store, a0, a1 in stores:
-                store(out_rows[:, a0:a1, v0 : v0 + w], result[:, a0:a1, :])
+            for queue, a0, a1 in stores:
+                queue.dma_start(out_rows[:, a0:a1, v0 : v0 + width], result[:, a0:a1, :])
 
-        WA, WB = 384, 128
-        diff_a = held.tile([P, PACK, WA], F32, name="diff_a", align_bytes=64)
-        late = []
+        early_diff = held.tile([P, PACK, EARLY], F32, name="early_diff", align_bytes=64)
+        late_right = []
         for t in range(PACK - 1):
             fetched = held.tile([P, V], F32, name="fetched%d" % t, align_bytes=64)
-            fetch_right(fetched[:, 0:WA], t, 0)
-            fetch_right(fetched[:, WA:V], t, WA)
-            subtract(diff_a[:, t, :], t, 0, fetched[:, 0:WA])
-            late.append(fetched[:, WA:V])
-        t = PACK - 1
-        first_half = held.tile([P, HALF], F32, name="first_half", tag="first_half_then_diff_b", align_bytes=64)
+            fetch_right(fetched[:, 0:EARLY], t, 0)
+            fetch_right(fetched[:, EARLY:V], t, EARLY)
+            subtract(early_diff[:, t, :], t, 0, fetched[:, 0:EARLY])
+            late_right.append(fetched[:, EARLY:V])
+        last = PACK - 1
+        first_half = held.tile([P, HALF], F32, name="first_half", tag="first_half_then_late_diff", align_bytes=64)
         second_half = held.tile([P, HALF], F32, name="second_half", align_bytes=64)
-        fetch_right(first_half[:], t, 0)
-        fetch_right(second_half[:], t, HALF)
-        subtract(diff_a[:, t, 0:HALF], t, 0, first_half[:])
-        subtract(diff_a[:, t, HALF:WA], t, HALF, second_half[:, 0 : WA - HALF])
-        late.append(second_half[:, WA - HALF : HALF])
+        fetch_right(first_half[:], last, 0)
+        fetch_right(second_half[:], last, HALF)
+        subtract(early_diff[:, last, 0:HALF], last, 0, first_half[:])
+        subtract(early_diff[:, last, HALF:EARLY], last, HALF, second_half[:, 0 : EARLY - HALF])
+        late_right.append(second_half[:, EARLY - HALF : HALF])
 
-        z_a0 = held.tile([P, HALF, PACK], BF16, name="z_a0", tag="z_first_last", align_bytes=64)
-        z_a1 = held.tile([P, WA - HALF, PACK], BF16, name="z_a1", align_bytes=64)
-        nc.scalar.activation(woven(z_a0[:]), planes(diff_a[:, :, 0:HALF]), RELU)
-        nc.scalar.activation(woven(z_a1[:]), planes(diff_a[:, :, HALF:WA]), RELU)
+        z_first = held.tile([P, HALF, PACK], BF16, name="z_first", tag="z_first_then_late", align_bytes=64)
+        z_middle = held.tile([P, EARLY - HALF, PACK], BF16, name="z_middle", align_bytes=64)
+        nc.scalar.activation(woven(z_first[:]), by_slot(early_diff[:, :, 0:HALF]), RELU)
+        nc.scalar.activation(woven(z_middle[:]), by_slot(early_diff[:, :, HALF:EARLY]), RELU)
 
-        diff_b = held.tile([P, PACK, WB], F32, name="diff_b", tag="first_half_then_diff_b", align_bytes=64)
+        late_diff = held.tile([P, PACK, V - EARLY], F32, name="late_diff", tag="first_half_then_late_diff", align_bytes=64)
         for t in range(PACK):
-            subtract(diff_b[:, t, :], t, WA, late[t])
+            subtract(late_diff[:, t, :], t, EARLY, late_right[t])
 
-        second_product((z_a0,), 0, (nc.scalar.copy, nc.scalar.copy), ((nc.sync.dma_start, 0, 2),))
-        z_b = held.tile([P, WB, PACK], BF16, name="z_b", tag="z_first_last", align_bytes=64)
-        nc.vector.tensor_scalar(woven(z_b[:]), planes(diff_b[:]), 0.0, None, MAX)
-        second_product((z_a1, z_b), HALF, (nc.scalar.copy, nc.vector.tensor_copy), ((nc.scalar.dma_start, 0, 1), (nc.sync.dma_start, 1, 2)))
+        second_product(z_first, 0, (nc.scalar.copy, nc.scalar.copy), ((nc.sync, 0, 1), (nc.sync, 1, 2)))
+        z_late = held.tile([P, V - EARLY, PACK], BF16, name="z_late", tag="z_first_then_late", align_bytes=64)
+        nc.vector.tensor_scalar(woven(z_late[:]), by_slot(late_diff[:]), 0.0, None, MAX)
+        second_product(z_middle, HALF, (nc.scalar.copy, nc.scalar.copy), ((nc.sync, 0, 2),))
+        second_product(z_late, EARLY, (nc.scalar.copy, nc.vector.tensor_copy), ((nc.scalar, 0, 1), (nc.sync, 1, 2)))

@@ -14,7 +14,6 @@ U8 = mybir.dt.uint8
 FP8X4 = mybir.dt.float8_e4m3fn_x4
 RELU = mybir.ActivationFunctionType.Relu
 SUBTRACT = mybir.AluOpType.subtract
-MAX = mybir.AluOpType.max
 
 P = 128
 PACK = 4
@@ -24,8 +23,8 @@ BLOCK_PARTITIONS = P // BLOCKS
 QUADRANT = 32
 BANK = 512
 RUN = 4
-HALF = V // 2
-EARLY = 3 * V // 4
+FIRST, SECOND, THIRD = V // 2, V // 4, V // 4
+PARTS = 2
 
 
 def tile_picked_phpair_relu_p_kernel(tc, x_words, x_scales, w1, w2, offs, left, right, out):
@@ -39,7 +38,7 @@ def tile_picked_phpair_relu_p_kernel(tc, x_words, x_scales, w1, w2, offs, left, 
         right_sb = held.tile([P, V // LIST], U16, name="right_sb")
         scale_table = held.tile([P, T], U8, name="scale_table", align_bytes=64)
         word_table = held.tile([P, T], U32, name="word_table", align_bytes=64)
-        w1_raw = [held.tile([P, PACK, H // 2], F32, name="w1_raw", tag="weights_raw%d" % c, align_bytes=64) for c in range(2)]
+        w1_raw = [held.tile([P, PACK, H // 2], F32, name="w1_raw", tag="slot%d" % (3 * c), align_bytes=64) for c in range(2)]
 
         scale_rows = x_scales[0].bitcast(I32).unsqueeze(1).to_broadcast([BLOCKS, BLOCK_PARTITIONS, T // 4])
         nc.sync.dma_start(scale_table[:].bitcast(I32), scale_rows)
@@ -48,46 +47,57 @@ def tile_picked_phpair_relu_p_kernel(tc, x_words, x_scales, w1, w2, offs, left, 
         w1_rows = w1.rearrange("(p j) c -> p j c", j=PACK)
         for c in range(2):
             nc.sync.dma_start(w1_raw[c][:], w1_rows[:, :, c * (H // 2) : (c + 1) * (H // 2)])
-        nc.sync.dma_start(right_sb[:], right)
-        nc.sync.dma_start(left_sb[:], left)
 
-        warm_in = held.tile([P, 1], F32, name="warm_in")
-        warm_out = held.tile([P, 1], F32, name="warm_out")
-        nc.vector.memset(warm_in[:], 0.0)
-        nc.scalar.activation(warm_out[:], warm_in[:], RELU)
+        def entries(list_sb, v0, count):
+            return list_sb[:, v0 // LIST : (v0 + count) // LIST]
 
         x_scale_rows = held.tile([P, S], U8, name="x_scale_rows", align_bytes=64)
         nc.vector.memset(x_scale_rows[:].bitcast(I32), 0)
         picked_scales = held.tile([P, S], U8, name="picked_scales", align_bytes=64)
         nc.vector.tensor_copy(picked_scales[:], scale_table[:].indirect(offs_sb[:]))
         for i in range(QUADRANT // BLOCK_PARTITIONS):
-            nc.scalar.dma_start(
+            nc.sync.dma_start(
                 x_scale_rows[i:P:QUADRANT, :].bitcast(I32),
                 picked_scales[BLOCK_PARTITIONS * i : P : QUADRANT, :].bitcast(I32),
             )
 
-        x_codes = held.tile([P, S], U32, name="x_codes", tag="x_codes_then_w2_bf", align_bytes=64)
+        nc.sync.dma_start(right_sb[:], right)
+        nc.sync.dma_start(left_sb[:], left)
+
+        x_codes = held.tile([P, S], U32, name="x_codes", tag="slot1", align_bytes=64)
         nc.vector.tensor_copy(x_codes[:], word_table[:].indirect(offs_sb[:]))
 
         w1_bf = held.tile([P, PACK, P, PACK], BF16, name="w1_bf", align_bytes=64)
         m_half = P // 2
-        shares = ((0, 0, m_half, nc.scalar.copy), (1, 0, m_half // 2, nc.scalar.copy), (1, m_half // 2, m_half, nc.vector.tensor_copy))
-        for c, m0, m1, copy in shares:
-            copy(
-                w1_bf[:, :, m_half * c + m0 : m_half * c + m1, :].rearrange("p t m j -> p m j t"),
-                w1_raw[c][:, :, PACK * m0 : PACK * m1].rearrange("p j (m t) -> p m j t", t=PACK),
+
+        def round_w1(c, t0, t1):
+            nc.scalar.copy(
+                w1_bf[:, t0:t1, m_half * c : m_half * (c + 1), :].rearrange("p t (g s) j -> p t g j s", s=RUN),
+                w1_raw[c][:].rearrange("p j (g t s) -> p t g j s", t=PACK, s=RUN)[:, t0:t1],
             )
-        w2_raw = held.tile([P, PACK, N], F32, name="w2_raw", tag="weights_raw0", align_bytes=64)
-        nc.sync.dma_start(w2_raw[:], w2.rearrange("(p j) n -> p j n", j=PACK))
+
+        round_w1(0, 0, PACK)
+        round_w1(1, 0, 1)
+        round_w1(1, 1, 2)
+        round_w1(1, 2, PACK)
+        w2_raw = held.tile([P, PACK, N], F32, name="w2_raw", tag="slot0", align_bytes=64)
+        w2_rows = w2.rearrange("(g t s) n -> t g s n", t=PACK, s=RUN)
+        for t in range(PACK):
+            nc.sync.dma_start(w2_raw[:, t, :], w2_rows[t])
 
         w1_codes = held.tile([P, H], U32, name="w1_codes", align_bytes=64)
         w1_scales = held.tile([P, H], U8, name="w1_scales", align_bytes=64)
-        for t0, t1 in ((0, 1), (1, 2), (2, PACK)):
+
+        def quantise_w1(t0, t1):
             nc.vector.quantize_mx(
                 out=w1_codes[:, t0 * P : t1 * P].bitcast(FP8X4),
                 scales=w1_scales[:, t0 * P : t1 * P],
                 in_=w1_bf[:, t0:t1, :, :].rearrange("p t m j -> p (t m j)"),
             )
+
+        quantise_w1(0, 1)
+        quantise_w1(1, 2)
+        quantise_w1(2, PACK)
 
         def woven(values):
             return values.rearrange("p (c r) t -> p c t r", r=RUN)
@@ -95,34 +105,33 @@ def tile_picked_phpair_relu_p_kernel(tc, x_words, x_scales, w1, w2, offs, left, 
         def by_slot(values):
             return values.rearrange("p t (c r) -> p c t r", r=RUN)
 
+        def first_pass(bank, t, c0, width):
+            nc.tensor.matmul_mx(
+                out=bank,
+                lhsT=w1_codes[:, t * P : (t + 1) * P].bitcast(FP8X4),
+                lhsT_scale=w1_scales[:, t * P : (t + 1) * P],
+                rhs=x_codes[:, c0 : c0 + width].bitcast(FP8X4),
+                rhs_scale=x_scale_rows[:, c0 : c0 + width],
+                start=True,
+                stop=True,
+            )
+
         h = []
+        quarter = S // 4
         for t in range(PACK):
             h_plane = held.tile([P, S], F32, name="h%d" % t, align_bytes=64)
-            width = BANK // 2 if t == 0 else BANK
-            for c0 in range(0, S, width):
-                cols = slice(c0, c0 + width)
+            width = quarter if t == 0 else BANK
+            for n, c0 in enumerate(range(0, S, width)):
                 bank = psum.tile([P, width], F32, name="bank")
-                nc.tensor.matmul_mx(
-                    out=bank[:],
-                    lhsT=w1_codes[:, t * P : (t + 1) * P].bitcast(FP8X4),
-                    lhsT_scale=w1_scales[:, t * P : (t + 1) * P],
-                    rhs=x_codes[:, cols].bitcast(FP8X4),
-                    rhs_scale=x_scale_rows[:, cols],
-                    start=True,
-                    stop=True,
-                )
-                nc.scalar.copy(h_plane[:, cols], bank[:])
+                first_pass(bank[:], t, c0, width)
+                copy = nc.vector.tensor_copy if t == 0 and n % 2 == 1 else nc.scalar.copy
+                copy(h_plane[:, c0 : c0 + width], bank[:])
             h.append(h_plane)
 
-        w2_bf = held.tile([P, N, PACK], BF16, name="w2_bf", tag="x_codes_then_w2_bf", align_bytes=64)
+        w2_bf = held.tile([P, N, PACK], BF16, name="w2_bf", tag="slot1", align_bytes=64)
         w2_codes = held.tile([P, N], U32, name="w2_codes", align_bytes=64)
         w2_scales = held.tile([P, N], U8, name="w2_scales", align_bytes=64)
         row_tiles = [slice(a * P, (a + 1) * P) for a in range(N // P)]
-        nc.scalar.copy(woven(w2_bf[:]), by_slot(w2_raw[:]))
-        nc.vector.quantize_mx(out=w2_codes[:].bitcast(FP8X4), scales=w2_scales[:], in_=w2_bf[:].rearrange("p n j -> p (n j)"))
-
-        def entries(list_sb, v0, count):
-            return list_sb[:, v0 // LIST : (v0 + count) // LIST]
 
         def fetch_right(fetched, t, v0):
             nc.vector.tensor_copy(fetched, h[t][:].indirect(entries(right_sb, v0, fetched.shape[1])))
@@ -130,13 +139,16 @@ def tile_picked_phpair_relu_p_kernel(tc, x_words, x_scales, w1, w2, offs, left, 
         def subtract(diff, t, v0, fetched):
             nc.vector.tensor_tensor(diff, h[t][:].indirect(entries(left_sb, v0, fetched.shape[1])), fetched, SUBTRACT)
 
+        def round_z(z_bf, diff):
+            nc.scalar.activation(woven(z_bf), by_slot(diff), RELU)
+
+        def quantise_z(codes, scales, z_bf):
+            nc.vector.quantize_mx(out=codes.bitcast(FP8X4), scales=scales, in_=z_bf.rearrange("p v t -> p (v t)"))
+
         out_rows = out.rearrange("(a p) v -> p a v", p=P)
 
-        def second_product(z_bf, v0, copies, stores):
-            width = z_bf.shape[1]
-            z_codes = held.tile([P, width], U32, name="z_codes%d" % v0, align_bytes=64)
-            z_scales = held.tile([P, width], U8, name="z_scales%d" % v0, align_bytes=64)
-            nc.vector.quantize_mx(out=z_codes[:].bitcast(FP8X4), scales=z_scales[:], in_=z_bf[:].rearrange("p v t -> p (v t)"))
+        def second_product(codes, scales, v0, copies, stores):
+            width = codes.shape[1]
             result = held.tile([P, N // P, width], F32, name="result%d" % v0, align_bytes=64)
             for a, copy in enumerate(copies):
                 bank = psum.tile([P, width], F32, name="bank")
@@ -144,8 +156,8 @@ def tile_picked_phpair_relu_p_kernel(tc, x_words, x_scales, w1, w2, offs, left, 
                     out=bank[:],
                     lhsT=w2_codes[:, row_tiles[a]].bitcast(FP8X4),
                     lhsT_scale=w2_scales[:, row_tiles[a]],
-                    rhs=z_codes[:].bitcast(FP8X4),
-                    rhs_scale=z_scales[:],
+                    rhs=codes.bitcast(FP8X4),
+                    rhs_scale=scales,
                     start=True,
                     stop=True,
                 )
@@ -153,34 +165,43 @@ def tile_picked_phpair_relu_p_kernel(tc, x_words, x_scales, w1, w2, offs, left, 
             for queue, a0, a1 in stores:
                 queue.dma_start(out_rows[:, a0:a1, v0 : v0 + width], result[:, a0:a1, :])
 
-        early_diff = held.tile([P, PACK, EARLY], F32, name="early_diff", align_bytes=64)
-        late_right = []
-        for t in range(PACK - 1):
-            fetched = held.tile([P, V], F32, name="fetched%d" % t, align_bytes=64)
-            fetch_right(fetched[:, 0:EARLY], t, 0)
-            fetch_right(fetched[:, EARLY:V], t, EARLY)
-            subtract(early_diff[:, t, :], t, 0, fetched[:, 0:EARLY])
-            late_right.append(fetched[:, EARLY:V])
-        last = PACK - 1
-        first_half = held.tile([P, HALF], F32, name="first_half", tag="first_half_then_late_diff", align_bytes=64)
-        second_half = held.tile([P, HALF], F32, name="second_half", align_bytes=64)
-        fetch_right(first_half[:], last, 0)
-        fetch_right(second_half[:], last, HALF)
-        subtract(early_diff[:, last, 0:HALF], last, 0, first_half[:])
-        subtract(early_diff[:, last, HALF:EARLY], last, HALF, second_half[:, 0 : EARLY - HALF])
-        late_right.append(second_half[:, EARLY - HALF : HALF])
+        z_bf = [held.tile([P, width, PACK], BF16, name="z_bf%d" % n, align_bytes=64) for n, width in enumerate((FIRST, SECOND, THIRD))]
+        z_codes = [held.tile([P, width], U32, name="z_codes%d" % n, align_bytes=64) for n, width in enumerate((FIRST, SECOND, THIRD))]
+        z_scales = [held.tile([P, width], U8, name="z_scales%d" % n, align_bytes=64) for n, width in enumerate((FIRST, SECOND, THIRD))]
 
-        z_first = held.tile([P, HALF, PACK], BF16, name="z_first", tag="z_first_then_late", align_bytes=64)
-        z_middle = held.tile([P, EARLY - HALF, PACK], BF16, name="z_middle", align_bytes=64)
-        nc.scalar.activation(woven(z_first[:]), by_slot(early_diff[:, :, 0:HALF]), RELU)
-        nc.scalar.activation(woven(z_middle[:]), by_slot(early_diff[:, :, HALF:EARLY]), RELU)
-
-        late_diff = held.tile([P, PACK, V - EARLY], F32, name="late_diff", tag="first_half_then_late_diff", align_bytes=64)
+        first_diff = held.tile([P, PACK, FIRST], F32, name="first_diff", tag="slot2", align_bytes=64)
+        second_right = []
         for t in range(PACK):
-            subtract(late_diff[:, t, :], t, EARLY, late_right[t])
+            fetched = held.tile([P, FIRST + SECOND], F32, name="fetched%d" % t, align_bytes=64)
+            fetch_right(fetched[:, 0:FIRST], t, 0)
+            fetch_right(fetched[:, FIRST:], t, FIRST)
+            subtract(first_diff[:, t, :], t, 0, fetched[:, 0:FIRST])
+            second_right.append(fetched[:, FIRST:])
 
-        second_product(z_first, 0, (nc.scalar.copy, nc.scalar.copy), ((nc.sync, 0, 1), (nc.sync, 1, 2)))
-        z_late = held.tile([P, V - EARLY, PACK], BF16, name="z_late", tag="z_first_then_late", align_bytes=64)
-        nc.vector.tensor_scalar(woven(z_late[:]), by_slot(late_diff[:]), 0.0, None, MAX)
-        second_product(z_middle, HALF, (nc.scalar.copy, nc.scalar.copy), ((nc.sync, 0, 2),))
-        second_product(z_late, EARLY, (nc.scalar.copy, nc.vector.tensor_copy), ((nc.scalar, 0, 1), (nc.sync, 1, 2)))
+        nc.scalar.copy(woven(w2_bf[:]), by_slot(w2_raw[:]))
+        nc.vector.quantize_mx(out=w2_codes[:].bitcast(FP8X4), scales=w2_scales[:], in_=w2_bf[:].rearrange("p n j -> p (n j)"))
+        round_z(z_bf[0][:], first_diff[:])
+
+        second_diff = held.tile([P, PACK, SECOND], F32, name="second_diff", tag="slot0", align_bytes=64)
+        for t in range(PACK):
+            subtract(second_diff[:, t, :], t, FIRST, second_right[t])
+        round_z(z_bf[1][:], second_diff[:])
+        quantise_z(z_codes[0][:], z_scales[0][:], z_bf[0][:])
+        second_product(z_codes[0][:], z_scales[0][:], 0, (nc.scalar.copy, nc.scalar.copy), ((nc.sync, 0, 2),))
+
+        third0 = FIRST + SECOND
+        third_right = held.tile([P, PACK, THIRD], F32, name="third_right", tag="slot2", align_bytes=64)
+        for t in range(PACK):
+            fetch_right(third_right[:, t, :], t, third0)
+        quantise_z(z_codes[1][:], z_scales[1][:], z_bf[1][:])
+        part = THIRD // PARTS
+        third_diff = held.tile([P, PARTS, PACK, part], F32, name="third_diff", tag="slot0", align_bytes=64)
+        for u in range(PARTS):
+            for t in range(PACK):
+                subtract(third_diff[:, u, t, :], t, third0 + u * part, third_right[:, t, u * part : (u + 1) * part])
+            round_z(z_bf[2][:, u * part : (u + 1) * part, :], third_diff[:, u, :, :])
+        second_product(z_codes[1][:], z_scales[1][:], FIRST, (nc.scalar.copy, nc.scalar.copy), ((nc.sync, 0, 2),))
+        for u in range(PARTS):
+            cols = slice(u * part, (u + 1) * part)
+            quantise_z(z_codes[2][:, cols], z_scales[2][:, cols], z_bf[2][:, cols, :])
+        second_product(z_codes[2][:], z_scales[2][:], third0, (nc.scalar.copy, nc.vector.tensor_copy), ((nc.scalar, 0, 1), (nc.sync, 1, 2)))

@@ -14,6 +14,7 @@ U8 = mybir.dt.uint8
 FP8X4 = mybir.dt.float8_e4m3fn_x4
 RELU = mybir.ActivationFunctionType.Relu
 SUBTRACT = mybir.AluOpType.subtract
+MAX = mybir.AluOpType.max
 
 P = 128
 PACK = 4
@@ -23,8 +24,10 @@ BLOCK_PARTITIONS = P // BLOCKS
 QUADRANT = 32
 BANK = 512
 RUN = 4
-FIRST, SECOND, THIRD = V // 2, V // 4, V // 4
-PARTS = 2
+HALF = V // 2
+EARLY = 3 * V // 4
+LATE_WORDS = S // 4
+W1_PIECES = ((0, H // 4), (H // 4, H // 2), (H // 2, H))
 
 
 def tile_picked_phpair_relu_p_kernel(tc, x_words, x_scales, w1, w2, offs, left, right, out):
@@ -38,15 +41,22 @@ def tile_picked_phpair_relu_p_kernel(tc, x_words, x_scales, w1, w2, offs, left, 
         right_sb = held.tile([P, V // LIST], U16, name="right_sb")
         scale_table = held.tile([P, T], U8, name="scale_table", align_bytes=64)
         word_table = held.tile([P, T], U32, name="word_table", align_bytes=64)
-        w1_raw = [held.tile([P, PACK, H // 2], F32, name="w1_raw", tag="slot%d" % (3 * c), align_bytes=64) for c in range(2)]
-
-        scale_rows = x_scales[0].bitcast(I32).unsqueeze(1).to_broadcast([BLOCKS, BLOCK_PARTITIONS, T // 4])
-        nc.sync.dma_start(scale_table[:].bitcast(I32), scale_rows)
-        nc.sync.dma_start(offs_sb[:], offs)
-        nc.sync.dma_start(word_table[:].bitcast(I32), x_words[0].rearrange("p n t -> p (n t)").bitcast(I32))
         w1_rows = w1.rearrange("(p j) c -> p j c", j=PACK)
-        for c in range(2):
-            nc.sync.dma_start(w1_raw[c][:], w1_rows[:, :, c * (H // 2) : (c + 1) * (H // 2)])
+        w1_raw = []
+        for n, (c0, c1) in enumerate(W1_PIECES):
+            w1_raw.append(held.tile([P, PACK, c1 - c0], F32, name="w1_raw", tag="w1_raw%d" % n, align_bytes=64))
+
+        def load_w1(n):
+            c0, c1 = W1_PIECES[n]
+            nc.sync.dma_start(w1_raw[n][:], w1_rows[:, :, c0:c1])
+
+        nc.vector.memset(scale_table[:].bitcast(I32), 0)
+        nc.sync.dma_start(offs_sb[:], offs)
+        load_w1(0)
+        nc.sync.dma_start(scale_table[0:P:BLOCK_PARTITIONS, :].bitcast(I32), x_scales[0].bitcast(I32))
+        nc.sync.dma_start(word_table[:].bitcast(I32), x_words[0].rearrange("p n t -> p (n t)").bitcast(I32))
+        load_w1(1)
+        load_w1(2)
 
         def entries(list_sb, v0, count):
             return list_sb[:, v0 // LIST : (v0 + count) // LIST]
@@ -64,23 +74,29 @@ def tile_picked_phpair_relu_p_kernel(tc, x_words, x_scales, w1, w2, offs, left, 
         nc.sync.dma_start(right_sb[:], right)
         nc.sync.dma_start(left_sb[:], left)
 
-        x_codes = held.tile([P, S], U32, name="x_codes", tag="slot1", align_bytes=64)
-        nc.vector.tensor_copy(x_codes[:], word_table[:].indirect(offs_sb[:]))
+        early = S - LATE_WORDS
+        early_codes = held.tile([P, early], U32, name="early_codes", align_bytes=64)
+        nc.vector.tensor_copy(early_codes[:], word_table[:].indirect(entries(offs_sb, 0, early)))
 
-        w1_bf = held.tile([P, PACK, P, PACK], BF16, name="w1_bf", align_bytes=64)
-        m_half = P // 2
+        w1_first = held.tile([P, 1, P, PACK], BF16, name="w1_first", tag="slot1", align_bytes=64)
+        w1_rest = held.tile([P, PACK - 1, P, PACK], BF16, name="w1_rest", align_bytes=64)
 
-        def round_w1(c, t0, t1):
+        def w1_bf(t0, t1):
+            return w1_first[:] if t0 == 0 else w1_rest[:, t0 - 1 : t1 - 1]
+
+        def round_w1(n, t0, t1):
+            c0, c1 = W1_PIECES[n]
             nc.scalar.copy(
-                w1_bf[:, t0:t1, m_half * c : m_half * (c + 1), :].rearrange("p t (g s) j -> p t g j s", s=RUN),
-                w1_raw[c][:].rearrange("p j (g t s) -> p t g j s", t=PACK, s=RUN)[:, t0:t1],
+                w1_bf(t0, t1)[:, :, c0 // PACK : c1 // PACK, :].rearrange("p t (g s) j -> p t g j s", s=RUN),
+                w1_raw[n][:].rearrange("p j (g t s) -> p t g j s", t=PACK, s=RUN)[:, t0:t1],
             )
 
-        round_w1(0, 0, PACK)
-        round_w1(1, 0, 1)
-        round_w1(1, 1, 2)
-        round_w1(1, 2, PACK)
-        w2_raw = held.tile([P, PACK, N], F32, name="w2_raw", tag="slot0", align_bytes=64)
+        for n in range(2):
+            round_w1(n, 0, 1)
+            round_w1(n, 1, PACK)
+        for t0, t1 in ((0, 1), (1, 2), (2, PACK)):
+            round_w1(2, t0, t1)
+        w2_raw = held.tile([P, PACK, N], F32, name="w2_raw", tag="w1_raw2", align_bytes=64)
         w2_rows = w2.rearrange("(g t s) n -> t g s n", t=PACK, s=RUN)
         for t in range(PACK):
             nc.sync.dma_start(w2_raw[:, t, :], w2_rows[t])
@@ -92,11 +108,13 @@ def tile_picked_phpair_relu_p_kernel(tc, x_words, x_scales, w1, w2, offs, left, 
             nc.vector.quantize_mx(
                 out=w1_codes[:, t0 * P : t1 * P].bitcast(FP8X4),
                 scales=w1_scales[:, t0 * P : t1 * P],
-                in_=w1_bf[:, t0:t1, :, :].rearrange("p t m j -> p (t m j)"),
+                in_=w1_bf(t0, t1).rearrange("p t m j -> p (t m j)"),
             )
 
         quantise_w1(0, 1)
         quantise_w1(1, 2)
+        late_codes = held.tile([P, LATE_WORDS], U32, name="late_codes", tag="slot1", align_bytes=64)
+        nc.vector.tensor_copy(late_codes[:], word_table[:].indirect(entries(offs_sb, early, LATE_WORDS)))
         quantise_w1(2, PACK)
 
         def woven(values):
@@ -106,11 +124,12 @@ def tile_picked_phpair_relu_p_kernel(tc, x_words, x_scales, w1, w2, offs, left, 
             return values.rearrange("p t (c r) -> p c t r", r=RUN)
 
         def first_pass(bank, t, c0, width):
+            codes = early_codes[:, c0 : c0 + width] if c0 < early else late_codes[:, c0 - early : c0 - early + width]
             nc.tensor.matmul_mx(
                 out=bank,
                 lhsT=w1_codes[:, t * P : (t + 1) * P].bitcast(FP8X4),
                 lhsT_scale=w1_scales[:, t * P : (t + 1) * P],
-                rhs=x_codes[:, c0 : c0 + width].bitcast(FP8X4),
+                rhs=codes.bitcast(FP8X4),
                 rhs_scale=x_scale_rows[:, c0 : c0 + width],
                 start=True,
                 stop=True,
@@ -120,11 +139,16 @@ def tile_picked_phpair_relu_p_kernel(tc, x_words, x_scales, w1, w2, offs, left, 
         quarter = S // 4
         for t in range(PACK):
             h_plane = held.tile([P, S], F32, name="h%d" % t, align_bytes=64)
-            width = quarter if t == 0 else BANK
-            for n, c0 in enumerate(range(0, S, width)):
+            widths = (quarter, quarter, quarter, quarter // 2, quarter // 2) if t == 0 else (BANK, BANK)
+            for n, width in enumerate(widths):
+                c0 = sum(widths[:n])
                 bank = psum.tile([P, width], F32, name="bank")
-                first_pass(bank[:], t, c0, width)
-                copy = nc.vector.tensor_copy if t == 0 and n % 2 == 1 else nc.scalar.copy
+                if c0 < early < c0 + width:
+                    first_pass(bank[:, 0 : early - c0], t, c0, early - c0)
+                    first_pass(bank[:, early - c0 : width], t, early, c0 + width - early)
+                else:
+                    first_pass(bank[:], t, c0, width)
+                copy = nc.vector.tensor_copy if t == 0 and n == 2 else nc.scalar.copy
                 copy(h_plane[:, c0 : c0 + width], bank[:])
             h.append(h_plane)
 
@@ -132,6 +156,8 @@ def tile_picked_phpair_relu_p_kernel(tc, x_words, x_scales, w1, w2, offs, left, 
         w2_codes = held.tile([P, N], U32, name="w2_codes", align_bytes=64)
         w2_scales = held.tile([P, N], U8, name="w2_scales", align_bytes=64)
         row_tiles = [slice(a * P, (a + 1) * P) for a in range(N // P)]
+        nc.scalar.copy(woven(w2_bf[:]), by_slot(w2_raw[:]))
+        nc.vector.quantize_mx(out=w2_codes[:].bitcast(FP8X4), scales=w2_scales[:], in_=w2_bf[:].rearrange("p n j -> p (n j)"))
 
         def fetch_right(fetched, t, v0):
             nc.vector.tensor_copy(fetched, h[t][:].indirect(entries(right_sb, v0, fetched.shape[1])))
@@ -139,16 +165,13 @@ def tile_picked_phpair_relu_p_kernel(tc, x_words, x_scales, w1, w2, offs, left, 
         def subtract(diff, t, v0, fetched):
             nc.vector.tensor_tensor(diff, h[t][:].indirect(entries(left_sb, v0, fetched.shape[1])), fetched, SUBTRACT)
 
-        def round_z(z_bf, diff):
-            nc.scalar.activation(woven(z_bf), by_slot(diff), RELU)
-
-        def quantise_z(codes, scales, z_bf):
-            nc.vector.quantize_mx(out=codes.bitcast(FP8X4), scales=scales, in_=z_bf.rearrange("p v t -> p (v t)"))
-
         out_rows = out.rearrange("(a p) v -> p a v", p=P)
 
-        def second_product(codes, scales, v0, copies, stores):
-            width = codes.shape[1]
+        def second_product(z_bf, v0, copies, stores):
+            width = z_bf.shape[1]
+            z_codes = held.tile([P, width], U32, name="z_codes%d" % v0, align_bytes=64)
+            z_scales = held.tile([P, width], U8, name="z_scales%d" % v0, align_bytes=64)
+            nc.vector.quantize_mx(out=z_codes[:].bitcast(FP8X4), scales=z_scales[:], in_=z_bf[:].rearrange("p v t -> p (v t)"))
             result = held.tile([P, N // P, width], F32, name="result%d" % v0, align_bytes=64)
             for a, copy in enumerate(copies):
                 bank = psum.tile([P, width], F32, name="bank")
@@ -156,8 +179,8 @@ def tile_picked_phpair_relu_p_kernel(tc, x_words, x_scales, w1, w2, offs, left, 
                     out=bank[:],
                     lhsT=w2_codes[:, row_tiles[a]].bitcast(FP8X4),
                     lhsT_scale=w2_scales[:, row_tiles[a]],
-                    rhs=codes.bitcast(FP8X4),
-                    rhs_scale=scales,
+                    rhs=z_codes[:].bitcast(FP8X4),
+                    rhs_scale=z_scales[:],
                     start=True,
                     stop=True,
                 )
@@ -165,43 +188,34 @@ def tile_picked_phpair_relu_p_kernel(tc, x_words, x_scales, w1, w2, offs, left, 
             for queue, a0, a1 in stores:
                 queue.dma_start(out_rows[:, a0:a1, v0 : v0 + width], result[:, a0:a1, :])
 
-        z_bf = [held.tile([P, width, PACK], BF16, name="z_bf%d" % n, align_bytes=64) for n, width in enumerate((FIRST, SECOND, THIRD))]
-        z_codes = [held.tile([P, width], U32, name="z_codes%d" % n, align_bytes=64) for n, width in enumerate((FIRST, SECOND, THIRD))]
-        z_scales = [held.tile([P, width], U8, name="z_scales%d" % n, align_bytes=64) for n, width in enumerate((FIRST, SECOND, THIRD))]
+        early_diff = held.tile([P, PACK, EARLY], F32, name="early_diff", align_bytes=64)
+        late_right = []
+        for t in range(PACK - 1):
+            fetched = held.tile([P, V], F32, name="fetched%d" % t, align_bytes=64)
+            fetch_right(fetched[:, 0:EARLY], t, 0)
+            fetch_right(fetched[:, EARLY:V], t, EARLY)
+            subtract(early_diff[:, t, :], t, 0, fetched[:, 0:EARLY])
+            late_right.append(fetched[:, EARLY:V])
+        last = PACK - 1
+        first_half = held.tile([P, HALF], F32, name="first_half", tag="first_half_then_late_diff", align_bytes=64)
+        second_half = held.tile([P, HALF], F32, name="second_half", align_bytes=64)
+        fetch_right(first_half[:], last, 0)
+        fetch_right(second_half[:], last, HALF)
+        subtract(early_diff[:, last, 0:HALF], last, 0, first_half[:])
+        subtract(early_diff[:, last, HALF:EARLY], last, HALF, second_half[:, 0 : EARLY - HALF])
+        late_right.append(second_half[:, EARLY - HALF : HALF])
 
-        first_diff = held.tile([P, PACK, FIRST], F32, name="first_diff", tag="slot2", align_bytes=64)
-        second_right = []
+        z_first = held.tile([P, HALF, PACK], BF16, name="z_first", tag="z_first_then_late", align_bytes=64)
+        z_middle = held.tile([P, EARLY - HALF, PACK], BF16, name="z_middle", align_bytes=64)
+        nc.scalar.activation(woven(z_first[:]), by_slot(early_diff[:, :, 0:HALF]), RELU)
+        nc.scalar.activation(woven(z_middle[:]), by_slot(early_diff[:, :, HALF:EARLY]), RELU)
+
+        late_diff = held.tile([P, PACK, V - EARLY], F32, name="late_diff", tag="first_half_then_late_diff", align_bytes=64)
         for t in range(PACK):
-            fetched = held.tile([P, FIRST + SECOND], F32, name="fetched%d" % t, align_bytes=64)
-            fetch_right(fetched[:, 0:FIRST], t, 0)
-            fetch_right(fetched[:, FIRST:], t, FIRST)
-            subtract(first_diff[:, t, :], t, 0, fetched[:, 0:FIRST])
-            second_right.append(fetched[:, FIRST:])
+            subtract(late_diff[:, t, :], t, EARLY, late_right[t])
 
-        nc.scalar.copy(woven(w2_bf[:]), by_slot(w2_raw[:]))
-        nc.vector.quantize_mx(out=w2_codes[:].bitcast(FP8X4), scales=w2_scales[:], in_=w2_bf[:].rearrange("p n j -> p (n j)"))
-        round_z(z_bf[0][:], first_diff[:])
-
-        second_diff = held.tile([P, PACK, SECOND], F32, name="second_diff", tag="slot0", align_bytes=64)
-        for t in range(PACK):
-            subtract(second_diff[:, t, :], t, FIRST, second_right[t])
-        round_z(z_bf[1][:], second_diff[:])
-        quantise_z(z_codes[0][:], z_scales[0][:], z_bf[0][:])
-        second_product(z_codes[0][:], z_scales[0][:], 0, (nc.scalar.copy, nc.scalar.copy), ((nc.sync, 0, 2),))
-
-        third0 = FIRST + SECOND
-        third_right = held.tile([P, PACK, THIRD], F32, name="third_right", tag="slot2", align_bytes=64)
-        for t in range(PACK):
-            fetch_right(third_right[:, t, :], t, third0)
-        quantise_z(z_codes[1][:], z_scales[1][:], z_bf[1][:])
-        part = THIRD // PARTS
-        third_diff = held.tile([P, PARTS, PACK, part], F32, name="third_diff", tag="slot0", align_bytes=64)
-        for u in range(PARTS):
-            for t in range(PACK):
-                subtract(third_diff[:, u, t, :], t, third0 + u * part, third_right[:, t, u * part : (u + 1) * part])
-            round_z(z_bf[2][:, u * part : (u + 1) * part, :], third_diff[:, u, :, :])
-        second_product(z_codes[1][:], z_scales[1][:], FIRST, (nc.scalar.copy, nc.scalar.copy), ((nc.sync, 0, 2),))
-        for u in range(PARTS):
-            cols = slice(u * part, (u + 1) * part)
-            quantise_z(z_codes[2][:, cols], z_scales[2][:, cols], z_bf[2][:, cols, :])
-        second_product(z_codes[2][:], z_scales[2][:], third0, (nc.scalar.copy, nc.vector.tensor_copy), ((nc.scalar, 0, 1), (nc.sync, 1, 2)))
+        second_product(z_first, 0, (nc.scalar.copy, nc.scalar.copy), ((nc.sync, 0, 1), (nc.sync, 1, 2)))
+        z_late = held.tile([P, V - EARLY, PACK], BF16, name="z_late", tag="z_first_then_late", align_bytes=64)
+        nc.vector.tensor_scalar(woven(z_late[:]), by_slot(late_diff[:]), 0.0, None, MAX)
+        second_product(z_middle, HALF, (nc.scalar.copy, nc.scalar.copy), ((nc.sync, 0, 2),))
+        second_product(z_late, EARLY, (nc.scalar.copy, nc.vector.tensor_copy), ((nc.scalar, 0, 1), (nc.sync, 1, 2)))

@@ -27,7 +27,8 @@ RUN = 4
 HALF = V // 2
 EARLY = 3 * V // 4
 LATE_WORDS = S // 4
-W1_PIECES = ((0, H // 4), (H // 4, H // 2), (H // 2, H))
+W1_AHEAD = 3 * H // 8
+W1_LAST = H // 4
 
 
 def tile_picked_phpair_relu_p_kernel(tc, x_words, x_scales, w1, w2, offs, left, right, out):
@@ -42,21 +43,17 @@ def tile_picked_phpair_relu_p_kernel(tc, x_words, x_scales, w1, w2, offs, left, 
         scale_table = held.tile([P, T], U8, name="scale_table", align_bytes=64)
         word_table = held.tile([P, T], U32, name="word_table", align_bytes=64)
         w1_rows = w1.rearrange("(p j) c -> p j c", j=PACK)
-        w1_raw = []
-        for n, (c0, c1) in enumerate(W1_PIECES):
-            w1_raw.append(held.tile([P, PACK, c1 - c0], F32, name="w1_raw", tag="w1_raw%d" % n, align_bytes=64))
-
-        def load_w1(n):
-            c0, c1 = W1_PIECES[n]
-            nc.sync.dma_start(w1_raw[n][:], w1_rows[:, :, c0:c1])
+        w1_ahead = held.tile([P, PACK, W1_AHEAD], F32, name="w1_ahead", align_bytes=64)
+        w1_behind = held.tile([P, PACK, H - W1_AHEAD], F32, name="w1_behind", align_bytes=64)
+        middle = H - W1_AHEAD - W1_LAST
 
         nc.vector.memset(scale_table[:].bitcast(I32), 0)
+        nc.sync.dma_start(w1_ahead[:], w1_rows[:, :, 0:W1_AHEAD])
         nc.sync.dma_start(offs_sb[:], offs)
-        load_w1(0)
         nc.sync.dma_start(scale_table[0:P:BLOCK_PARTITIONS, :].bitcast(I32), x_scales[0].bitcast(I32))
         nc.sync.dma_start(word_table[:].bitcast(I32), x_words[0].rearrange("p n t -> p (n t)").bitcast(I32))
-        load_w1(1)
-        load_w1(2)
+        nc.sync.dma_start(w1_behind[:, :, 0:middle], w1_rows[:, :, W1_AHEAD : H - W1_LAST])
+        nc.sync.dma_start(w1_behind[:, :, middle:], w1_rows[:, :, H - W1_LAST : H])
 
         def entries(list_sb, v0, count):
             return list_sb[:, v0 // LIST : (v0 + count) // LIST]
@@ -84,19 +81,21 @@ def tile_picked_phpair_relu_p_kernel(tc, x_words, x_scales, w1, w2, offs, left, 
         def w1_bf(t0, t1):
             return w1_first[:] if t0 == 0 else w1_rest[:, t0 - 1 : t1 - 1]
 
-        def round_w1(n, t0, t1):
-            c0, c1 = W1_PIECES[n]
+        def round_w1(raw, c0, t0, t1):
+            c1 = c0 + raw.shape[2]
             nc.scalar.copy(
                 w1_bf(t0, t1)[:, :, c0 // PACK : c1 // PACK, :].rearrange("p t (g s) j -> p t g j s", s=RUN),
-                w1_raw[n][:].rearrange("p j (g t s) -> p t g j s", t=PACK, s=RUN)[:, t0:t1],
+                raw.rearrange("p j (g t s) -> p t g j s", t=PACK, s=RUN)[:, t0:t1],
             )
 
-        for n in range(2):
-            round_w1(n, 0, 1)
-            round_w1(n, 1, PACK)
-        for t0, t1 in ((0, 1), (1, 2), (2, PACK)):
-            round_w1(2, t0, t1)
-        w2_raw = held.tile([P, PACK, N], F32, name="w2_raw", tag="w1_raw2", align_bytes=64)
+        round_w1(w1_ahead[:], 0, 0, 1)
+        round_w1(w1_ahead[:], 0, 1, PACK)
+        for t in range(2):
+            round_w1(w1_behind[:, :, 0:middle], W1_AHEAD, t, t + 1)
+        for t in range(2):
+            round_w1(w1_behind[:, :, middle:], H - W1_LAST, t, t + 1)
+        round_w1(w1_behind[:], W1_AHEAD, 2, PACK)
+        w2_raw = held.tile([P, PACK, N], F32, name="w2_raw", tag="w1_behind", align_bytes=64)
         w2_rows = w2.rearrange("(g t s) n -> t g s n", t=PACK, s=RUN)
         for t in range(PACK):
             nc.sync.dma_start(w2_raw[:, t, :], w2_rows[t])

@@ -22,13 +22,19 @@ LIST = 16
 BLOCKS = K // 32
 BLOCK_PARTITIONS = P // BLOCKS
 QUADRANT = 32
+QUADRANT_ROWS = QUADRANT // BLOCK_PARTITIONS
 BANK = 512
 RUN = 4
+
+EARLY_PLACES = 3 * S // 4
+LATE_PLACES = S - EARLY_PLACES
+W1_AHEAD = H // 4
+W1_LAST = H // 4
+W1_MIDDLE = H - W1_AHEAD - W1_LAST
+PLANE_0_WIDTHS = (S // 4, S // 4, S // 4, S // 8, S // 8)
+VECTOR_BANK = 2
 HALF = V // 2
 EARLY = 3 * V // 4
-LATE_WORDS = S // 4
-W1_AHEAD = 3 * H // 8
-W1_LAST = H // 4
 
 
 def tile_picked_phpair_relu_p_kernel(tc, x_words, x_scales, w1, w2, offs, left, right, out):
@@ -45,37 +51,41 @@ def tile_picked_phpair_relu_p_kernel(tc, x_words, x_scales, w1, w2, offs, left, 
         w1_rows = w1.rearrange("(p j) c -> p j c", j=PACK)
         w1_ahead = held.tile([P, PACK, W1_AHEAD], F32, name="w1_ahead", align_bytes=64)
         w1_behind = held.tile([P, PACK, H - W1_AHEAD], F32, name="w1_behind", align_bytes=64)
-        middle = H - W1_AHEAD - W1_LAST
 
         nc.vector.memset(scale_table[:].bitcast(I32), 0)
         nc.sync.dma_start(w1_ahead[:], w1_rows[:, :, 0:W1_AHEAD])
         nc.sync.dma_start(offs_sb[:], offs)
+        nc.sync.dma_start(right_sb[:], right)
+        nc.sync.dma_start(left_sb[:], left)
         nc.sync.dma_start(scale_table[0:P:BLOCK_PARTITIONS, :].bitcast(I32), x_scales[0].bitcast(I32))
         nc.sync.dma_start(word_table[:].bitcast(I32), x_words[0].rearrange("p n t -> p (n t)").bitcast(I32))
-        nc.sync.dma_start(w1_behind[:, :, 0:middle], w1_rows[:, :, W1_AHEAD : H - W1_LAST])
-        nc.sync.dma_start(w1_behind[:, :, middle:], w1_rows[:, :, H - W1_LAST : H])
+        nc.sync.dma_start(w1_behind[:, :, 0:W1_MIDDLE], w1_rows[:, :, W1_AHEAD : H - W1_LAST])
+        nc.sync.dma_start(w1_behind[:, :, W1_MIDDLE:], w1_rows[:, :, H - W1_LAST : H])
 
         def entries(list_sb, v0, count):
             return list_sb[:, v0 // LIST : (v0 + count) // LIST]
 
-        x_scale_rows = held.tile([P, S], U8, name="x_scale_rows", align_bytes=64)
-        nc.vector.memset(x_scale_rows[:].bitcast(I32), 0)
-        picked_scales = held.tile([P, S], U8, name="picked_scales", align_bytes=64)
-        nc.vector.tensor_copy(picked_scales[:], scale_table[:].indirect(offs_sb[:]))
-        for i in range(QUADRANT // BLOCK_PARTITIONS):
-            nc.sync.dma_start(
-                x_scale_rows[i:P:QUADRANT, :].bitcast(I32),
-                picked_scales[BLOCK_PARTITIONS * i : P : QUADRANT, :].bitcast(I32),
-            )
+        def pick_scales(c0, count):
+            picked = held.tile([P, count], U8, name="picked%d" % c0, align_bytes=64)
+            nc.vector.tensor_copy(picked[:], scale_table[:].indirect(entries(offs_sb, c0, count)))
+            return picked
 
-        nc.sync.dma_start(right_sb[:], right)
-        nc.sync.dma_start(left_sb[:], left)
+        def move_rows(rows, picked, first_row):
+            for r in range(first_row, QUADRANT_ROWS):
+                nc.sync.dma_start(rows[r:P:QUADRANT, :].bitcast(I32), picked[BLOCK_PARTITIONS * r : P : QUADRANT, :].bitcast(I32))
 
-        early = S - LATE_WORDS
-        early_codes = held.tile([P, early], U32, name="early_codes", align_bytes=64)
-        nc.vector.tensor_copy(early_codes[:], word_table[:].indirect(entries(offs_sb, 0, early)))
+        early_rows = held.tile([P, EARLY_PLACES], U8, name="early_rows", align_bytes=64)
+        nc.vector.memset(early_rows[:].bitcast(I32), 0)
+        move_rows(early_rows, pick_scales(0, EARLY_PLACES), 0)
+        late_rows = held.tile([P, LATE_PLACES], U8, name="late_rows", align_bytes=64)
+        late_picked = pick_scales(EARLY_PLACES, LATE_PLACES)
+        nc.vector.tensor_copy(late_rows[:].bitcast(I32), late_picked[:].bitcast(I32))
+        move_rows(late_rows, late_picked, 1)
 
-        w1_first = held.tile([P, 1, P, PACK], BF16, name="w1_first", tag="slot1", align_bytes=64)
+        early_codes = held.tile([P, EARLY_PLACES], U32, name="early_codes", align_bytes=64)
+        nc.vector.tensor_copy(early_codes[:], word_table[:].indirect(entries(offs_sb, 0, EARLY_PLACES)))
+
+        w1_first = held.tile([P, 1, P, PACK], BF16, name="w1_first", tag="reused", align_bytes=64)
         w1_rest = held.tile([P, PACK - 1, P, PACK], BF16, name="w1_rest", align_bytes=64)
 
         def w1_bf(t0, t1):
@@ -90,11 +100,12 @@ def tile_picked_phpair_relu_p_kernel(tc, x_words, x_scales, w1, w2, offs, left, 
 
         round_w1(w1_ahead[:], 0, 0, 1)
         round_w1(w1_ahead[:], 0, 1, PACK)
-        for t in range(2):
-            round_w1(w1_behind[:, :, 0:middle], W1_AHEAD, t, t + 1)
-        for t in range(2):
-            round_w1(w1_behind[:, :, middle:], H - W1_LAST, t, t + 1)
+        for t in (0, 1):
+            round_w1(w1_behind[:, :, 0:W1_MIDDLE], W1_AHEAD, t, t + 1)
+        for t in (0, 1):
+            round_w1(w1_behind[:, :, W1_MIDDLE:], H - W1_LAST, t, t + 1)
         round_w1(w1_behind[:], W1_AHEAD, 2, PACK)
+
         w2_raw = held.tile([P, PACK, N], F32, name="w2_raw", tag="w1_behind", align_bytes=64)
         w2_rows = w2.rearrange("(g t s) n -> t g s n", t=PACK, s=RUN)
         for t in range(PACK):
@@ -112,8 +123,8 @@ def tile_picked_phpair_relu_p_kernel(tc, x_words, x_scales, w1, w2, offs, left, 
 
         quantise_w1(0, 1)
         quantise_w1(1, 2)
-        late_codes = held.tile([P, LATE_WORDS], U32, name="late_codes", tag="slot1", align_bytes=64)
-        nc.vector.tensor_copy(late_codes[:], word_table[:].indirect(entries(offs_sb, early, LATE_WORDS)))
+        late_codes = held.tile([P, LATE_PLACES], U32, name="late_codes", tag="reused", align_bytes=64)
+        nc.vector.tensor_copy(late_codes[:], word_table[:].indirect(entries(offs_sb, EARLY_PLACES, LATE_PLACES)))
         quantise_w1(2, PACK)
 
         def woven(values):
@@ -123,35 +134,34 @@ def tile_picked_phpair_relu_p_kernel(tc, x_words, x_scales, w1, w2, offs, left, 
             return values.rearrange("p t (c r) -> p c t r", r=RUN)
 
         def first_pass(bank, t, c0, width):
-            codes = early_codes[:, c0 : c0 + width] if c0 < early else late_codes[:, c0 - early : c0 - early + width]
+            codes, rows, x0 = (early_codes, early_rows, c0) if c0 < EARLY_PLACES else (late_codes, late_rows, c0 - EARLY_PLACES)
             nc.tensor.matmul_mx(
                 out=bank,
                 lhsT=w1_codes[:, t * P : (t + 1) * P].bitcast(FP8X4),
                 lhsT_scale=w1_scales[:, t * P : (t + 1) * P],
-                rhs=codes.bitcast(FP8X4),
-                rhs_scale=x_scale_rows[:, c0 : c0 + width],
+                rhs=codes[:, x0 : x0 + width].bitcast(FP8X4),
+                rhs_scale=rows[:, x0 : x0 + width],
                 start=True,
                 stop=True,
             )
 
         h = []
-        quarter = S // 4
         for t in range(PACK):
             h_plane = held.tile([P, S], F32, name="h%d" % t, align_bytes=64)
-            widths = (quarter, quarter, quarter, quarter // 2, quarter // 2) if t == 0 else (BANK, BANK)
+            widths = PLANE_0_WIDTHS if t == 0 else (BANK, BANK)
             for n, width in enumerate(widths):
                 c0 = sum(widths[:n])
                 bank = psum.tile([P, width], F32, name="bank")
-                if c0 < early < c0 + width:
-                    first_pass(bank[:, 0 : early - c0], t, c0, early - c0)
-                    first_pass(bank[:, early - c0 : width], t, early, c0 + width - early)
+                if c0 < EARLY_PLACES < c0 + width:
+                    first_pass(bank[:, 0 : EARLY_PLACES - c0], t, c0, EARLY_PLACES - c0)
+                    first_pass(bank[:, EARLY_PLACES - c0 : width], t, EARLY_PLACES, c0 + width - EARLY_PLACES)
                 else:
                     first_pass(bank[:], t, c0, width)
-                copy = nc.vector.tensor_copy if t == 0 and n == 2 else nc.scalar.copy
+                copy = nc.vector.tensor_copy if t == 0 and n == VECTOR_BANK else nc.scalar.copy
                 copy(h_plane[:, c0 : c0 + width], bank[:])
             h.append(h_plane)
 
-        w2_bf = held.tile([P, N, PACK], BF16, name="w2_bf", tag="slot1", align_bytes=64)
+        w2_bf = held.tile([P, N, PACK], BF16, name="w2_bf", tag="reused", align_bytes=64)
         w2_codes = held.tile([P, N], U32, name="w2_codes", align_bytes=64)
         w2_scales = held.tile([P, N], U8, name="w2_scales", align_bytes=64)
         row_tiles = [slice(a * P, (a + 1) * P) for a in range(N // P)]

@@ -55,8 +55,6 @@ def tile_picked_phpair_relu_p_kernel(tc, x_words, x_scales, w1, w2, offs, left, 
         nc.vector.memset(scale_table[:].bitcast(I32), 0)
         nc.sync.dma_start(w1_ahead[:], w1_rows[:, :, 0:W1_AHEAD])
         nc.sync.dma_start(offs_sb[:], offs)
-        nc.sync.dma_start(right_sb[:], right)
-        nc.sync.dma_start(left_sb[:], left)
         nc.sync.dma_start(scale_table[0:P:BLOCK_PARTITIONS, :].bitcast(I32), x_scales[0].bitcast(I32))
         nc.sync.dma_start(word_table[:].bitcast(I32), x_words[0].rearrange("p n t -> p (n t)").bitcast(I32))
         nc.sync.dma_start(w1_behind[:, :, 0:W1_MIDDLE], w1_rows[:, :, W1_AHEAD : H - W1_LAST])
@@ -65,22 +63,18 @@ def tile_picked_phpair_relu_p_kernel(tc, x_words, x_scales, w1, w2, offs, left, 
         def entries(list_sb, v0, count):
             return list_sb[:, v0 // LIST : (v0 + count) // LIST]
 
-        def pick_scales(c0, count):
-            picked = held.tile([P, count], U8, name="picked%d" % c0, align_bytes=64)
-            nc.vector.tensor_copy(picked[:], scale_table[:].indirect(entries(offs_sb, c0, count)))
-            return picked
+        x_scale_rows = held.tile([P, S], U8, name="x_scale_rows", align_bytes=64)
+        nc.vector.memset(x_scale_rows[:].bitcast(I32), 0)
+        picked_scales = held.tile([P, S], U8, name="picked_scales", align_bytes=64)
+        nc.vector.tensor_copy(picked_scales[:], scale_table[:].indirect(offs_sb[:]))
+        for r in range(QUADRANT_ROWS):
+            nc.sync.dma_start(
+                x_scale_rows[r:P:QUADRANT, :].bitcast(I32),
+                picked_scales[BLOCK_PARTITIONS * r : P : QUADRANT, :].bitcast(I32),
+            )
 
-        def move_rows(rows, picked, first_row):
-            for r in range(first_row, QUADRANT_ROWS):
-                nc.sync.dma_start(rows[r:P:QUADRANT, :].bitcast(I32), picked[BLOCK_PARTITIONS * r : P : QUADRANT, :].bitcast(I32))
-
-        early_rows = held.tile([P, EARLY_PLACES], U8, name="early_rows", align_bytes=64)
-        nc.vector.memset(early_rows[:].bitcast(I32), 0)
-        move_rows(early_rows, pick_scales(0, EARLY_PLACES), 0)
-        late_rows = held.tile([P, LATE_PLACES], U8, name="late_rows", align_bytes=64)
-        late_picked = pick_scales(EARLY_PLACES, LATE_PLACES)
-        nc.vector.tensor_copy(late_rows[:].bitcast(I32), late_picked[:].bitcast(I32))
-        move_rows(late_rows, late_picked, 1)
+        nc.sync.dma_start(right_sb[:], right)
+        nc.sync.dma_start(left_sb[:], left)
 
         early_codes = held.tile([P, EARLY_PLACES], U32, name="early_codes", align_bytes=64)
         nc.vector.tensor_copy(early_codes[:], word_table[:].indirect(entries(offs_sb, 0, EARLY_PLACES)))
@@ -134,13 +128,13 @@ def tile_picked_phpair_relu_p_kernel(tc, x_words, x_scales, w1, w2, offs, left, 
             return values.rearrange("p t (c r) -> p c t r", r=RUN)
 
         def first_pass(bank, t, c0, width):
-            codes, rows, x0 = (early_codes, early_rows, c0) if c0 < EARLY_PLACES else (late_codes, late_rows, c0 - EARLY_PLACES)
+            codes, x0 = (early_codes, c0) if c0 < EARLY_PLACES else (late_codes, c0 - EARLY_PLACES)
             nc.tensor.matmul_mx(
                 out=bank,
                 lhsT=w1_codes[:, t * P : (t + 1) * P].bitcast(FP8X4),
                 lhsT_scale=w1_scales[:, t * P : (t + 1) * P],
                 rhs=codes[:, x0 : x0 + width].bitcast(FP8X4),
-                rhs_scale=rows[:, x0 : x0 + width],
+                rhs_scale=x_scale_rows[:, c0 : c0 + width],
                 start=True,
                 stop=True,
             )

@@ -13,6 +13,7 @@ U16 = mybir.dt.uint16
 U8 = mybir.dt.uint8
 FP8X4 = mybir.dt.float8_e4m3fn_x4
 RELU = mybir.ActivationFunctionType.Relu
+COPY = mybir.ActivationFunctionType.Copy
 SUBTRACT = mybir.AluOpType.subtract
 MAX = mybir.AluOpType.max
 
@@ -60,6 +61,9 @@ def tile_picked_phpair_relu_p_kernel(tc, x_words, x_scales, w1, w2, offs, left, 
         nc.sync.dma_start(w1_behind[:, :, 0:W1_MIDDLE], w1_rows[:, :, W1_AHEAD : H - W1_LAST])
         nc.sync.dma_start(w1_behind[:, :, W1_MIDDLE:], w1_rows[:, :, H - W1_LAST : H])
 
+        nc.sync.dma_start(right_sb[:], right)
+        nc.sync.dma_start(left_sb[:], left)
+
         def entries(list_sb, v0, count):
             return list_sb[:, v0 // LIST : (v0 + count) // LIST]
 
@@ -72,9 +76,6 @@ def tile_picked_phpair_relu_p_kernel(tc, x_words, x_scales, w1, w2, offs, left, 
                 x_scale_rows[r:P:QUADRANT, :].bitcast(I32),
                 picked_scales[BLOCK_PARTITIONS * r : P : QUADRANT, :].bitcast(I32),
             )
-
-        nc.sync.dma_start(right_sb[:], right)
-        nc.sync.dma_start(left_sb[:], left)
 
         early_codes = held.tile([P, EARLY_PLACES], U32, name="early_codes", align_bytes=64)
         nc.vector.tensor_copy(early_codes[:], word_table[:].indirect(entries(offs_sb, 0, EARLY_PLACES)))
@@ -100,7 +101,7 @@ def tile_picked_phpair_relu_p_kernel(tc, x_words, x_scales, w1, w2, offs, left, 
             round_w1(w1_behind[:, :, W1_MIDDLE:], H - W1_LAST, t, t + 1)
         round_w1(w1_behind[:], W1_AHEAD, 2, PACK)
 
-        w2_raw = held.tile([P, PACK, N], F32, name="w2_raw", tag="w1_behind", align_bytes=64)
+        w2_raw = held.tile([P, PACK, N], F32, name="w2_raw", tag="scale_table", align_bytes=64)
         w2_rows = w2.rearrange("(g t s) n -> t g s n", t=PACK, s=RUN)
         for t in range(PACK):
             nc.sync.dma_start(w2_raw[:, t, :], w2_rows[t])
@@ -127,6 +128,13 @@ def tile_picked_phpair_relu_p_kernel(tc, x_words, x_scales, w1, w2, offs, left, 
         def by_slot(values):
             return values.rearrange("p t (c r) -> p c t r", r=RUN)
 
+        w2_bf = held.tile([P, N, PACK], BF16, name="w2_bf", align_bytes=64)
+        w2_codes = held.tile([P, N], U32, name="w2_codes", align_bytes=64)
+        w2_scales = held.tile([P, N], U8, name="w2_scales", align_bytes=64)
+        row_tiles = [slice(a * P, (a + 1) * P) for a in range(N // P)]
+        nc.vector.tensor_copy(woven(w2_bf[:]), by_slot(w2_raw[:]))
+        nc.vector.quantize_mx(out=w2_codes[:].bitcast(FP8X4), scales=w2_scales[:], in_=w2_bf[:].rearrange("p n j -> p (n j)"))
+
         def first_pass(bank, t, c0, width):
             codes, x0 = (early_codes, c0) if c0 < EARLY_PLACES else (late_codes, c0 - EARLY_PLACES)
             nc.tensor.matmul_mx(
@@ -140,6 +148,7 @@ def tile_picked_phpair_relu_p_kernel(tc, x_words, x_scales, w1, w2, offs, left, 
             )
 
         h = []
+        last_banks = []
         for t in range(PACK):
             h_plane = held.tile([P, S], F32, name="h%d" % t, align_bytes=64)
             widths = PLANE_0_WIDTHS if t == 0 else (BANK, BANK)
@@ -151,19 +160,19 @@ def tile_picked_phpair_relu_p_kernel(tc, x_words, x_scales, w1, w2, offs, left, 
                     first_pass(bank[:, EARLY_PLACES - c0 : width], t, EARLY_PLACES, c0 + width - EARLY_PLACES)
                 else:
                     first_pass(bank[:], t, c0, width)
-                copy = nc.vector.tensor_copy if t == 0 and n == VECTOR_BANK else nc.scalar.copy
-                copy(h_plane[:, c0 : c0 + width], bank[:])
+                if t == PACK - 1:
+                    last_banks.append((c0, width, bank))
+                else:
+                    copy = nc.vector.tensor_copy if t == 0 and n == VECTOR_BANK else nc.scalar.copy
+                    copy(h_plane[:, c0 : c0 + width], bank[:])
             h.append(h_plane)
 
-        w2_bf = held.tile([P, N, PACK], BF16, name="w2_bf", tag="reused", align_bytes=64)
-        w2_codes = held.tile([P, N], U32, name="w2_codes", align_bytes=64)
-        w2_scales = held.tile([P, N], U8, name="w2_scales", align_bytes=64)
-        row_tiles = [slice(a * P, (a + 1) * P) for a in range(N // P)]
-        nc.scalar.copy(woven(w2_bf[:]), by_slot(w2_raw[:]))
-        nc.vector.quantize_mx(out=w2_codes[:].bitcast(FP8X4), scales=w2_scales[:], in_=w2_bf[:].rearrange("p n j -> p (n j)"))
-
         def fetch_right(fetched, t, v0):
-            nc.vector.tensor_copy(fetched, h[t][:].indirect(entries(right_sb, v0, fetched.shape[1])))
+            window = h[t][:].indirect(entries(right_sb, v0, fetched.shape[1]))
+            if t == 0:
+                nc.vector.tensor_copy(fetched, window)
+            else:
+                nc.scalar.activation(fetched, window, COPY)
 
         def subtract(diff, t, v0, fetched):
             nc.vector.tensor_tensor(diff, h[t][:].indirect(entries(left_sb, v0, fetched.shape[1])), fetched, SUBTRACT)
@@ -195,10 +204,16 @@ def tile_picked_phpair_relu_p_kernel(tc, x_words, x_scales, w1, w2, offs, left, 
         late_right = []
         for t in range(PACK - 1):
             fetched = held.tile([P, V], F32, name="fetched%d" % t, align_bytes=64)
-            fetch_right(fetched[:, 0:EARLY], t, 0)
-            fetch_right(fetched[:, EARLY:V], t, EARLY)
+            if t == 0:
+                fetch_right(fetched[:, 0:EARLY], t, 0)
+                fetch_right(fetched[:, EARLY:V], t, EARLY)
+            else:
+                fetch_right(fetched[:], t, 0)
             subtract(early_diff[:, t, :], t, 0, fetched[:, 0:EARLY])
             late_right.append(fetched[:, EARLY:V])
+            if t == 0:
+                for c0, width, bank in last_banks:
+                    nc.vector.tensor_copy(h[PACK - 1][:, c0 : c0 + width], bank[:])
         last = PACK - 1
         first_half = held.tile([P, HALF], F32, name="first_half", tag="first_half_then_late_diff", align_bytes=64)
         second_half = held.tile([P, HALF], F32, name="second_half", align_bytes=64)

@@ -16,6 +16,8 @@ RELU = mybir.ActivationFunctionType.Relu
 COPY = mybir.ActivationFunctionType.Copy
 SUBTRACT = mybir.AluOpType.subtract
 MAX = mybir.AluOpType.max
+MULT = mybir.AluOpType.mult
+ADD = mybir.AluOpType.add
 
 P = 128
 PACK = 4
@@ -128,12 +130,8 @@ def tile_picked_phpair_relu_p_kernel(tc, x_words, x_scales, w1, w2, offs, left, 
         def by_slot(values):
             return values.rearrange("p t (c r) -> p c t r", r=RUN)
 
-        w2_bf = held.tile([P, N, PACK], BF16, name="w2_bf", align_bytes=64)
-        w2_codes = held.tile([P, N], U32, name="w2_codes", align_bytes=64)
         w2_scales = held.tile([P, N], U8, name="w2_scales", align_bytes=64)
         row_tiles = [slice(a * P, (a + 1) * P) for a in range(N // P)]
-        nc.vector.tensor_copy(woven(w2_bf[:]), by_slot(w2_raw[:]))
-        nc.vector.quantize_mx(out=w2_codes[:].bitcast(FP8X4), scales=w2_scales[:], in_=w2_bf[:].rearrange("p n j -> p (n j)"))
 
         def first_pass(bank, t, c0, width):
             codes, x0 = (early_codes, c0) if c0 < EARLY_PLACES else (late_codes, c0 - EARLY_PLACES)
@@ -167,9 +165,9 @@ def tile_picked_phpair_relu_p_kernel(tc, x_words, x_scales, w1, w2, offs, left, 
                     copy(h_plane[:, c0 : c0 + width], bank[:])
             h.append(h_plane)
 
-        def fetch_right(fetched, t, v0):
+        def fetch_right(on_vector, fetched, t, v0):
             window = h[t][:].indirect(entries(right_sb, v0, fetched.shape[1]))
-            if t == 0:
+            if on_vector:
                 nc.vector.tensor_copy(fetched, window)
             else:
                 nc.scalar.activation(fetched, window, COPY)
@@ -201,26 +199,33 @@ def tile_picked_phpair_relu_p_kernel(tc, x_words, x_scales, w1, w2, offs, left, 
                 queue.dma_start(out_rows[:, a0:a1, v0 : v0 + width], result[:, a0:a1, :])
 
         early_diff = held.tile([P, PACK, EARLY], F32, name="early_diff", align_bytes=64)
-        late_right = []
         for t in range(PACK - 1):
-            fetched = held.tile([P, V], F32, name="fetched%d" % t, align_bytes=64)
+            fetched = held.tile([P, EARLY], F32, name="fetched%d" % t, align_bytes=64)
             if t == 0:
-                fetch_right(fetched[:, 0:EARLY], t, 0)
-                fetch_right(fetched[:, EARLY:V], t, EARLY)
+                fetch_right(True, fetched[:], t, 0)
+                late_first = held.tile([P, V - EARLY], F32, name="late_first", align_bytes=64)
+                fetch_right(True, late_first[:], t, EARLY)
             else:
-                fetch_right(fetched[:], t, 0)
-            subtract(early_diff[:, t, :], t, 0, fetched[:, 0:EARLY])
-            late_right.append(fetched[:, EARLY:V])
+                fetch_right(False, fetched[:], t, 0)
+            subtract(early_diff[:, t, :], t, 0, fetched[:])
             if t == 0:
+                w2_bf = held.tile([P, N, PACK], BF16, name="w2_bf", tag="fetched0", align_bytes=64)
+                nc.gpsimd.tensor_scalar(w2_bf[:], w2_raw[:].rearrange("p t n -> p n t"), 1.0, 0.0, MULT, ADD)
                 for c0, width, bank in last_banks:
                     nc.vector.tensor_copy(h[PACK - 1][:, c0 : c0 + width], bank[:])
         last = PACK - 1
         first_half = held.tile([P, HALF], F32, name="first_half", tag="first_half_then_late_diff", align_bytes=64)
         second_half = held.tile([P, HALF], F32, name="second_half", align_bytes=64)
-        fetch_right(first_half[:], last, 0)
-        fetch_right(second_half[:], last, HALF)
+        fetch_right(False, first_half[:], last, 0)
+        fetch_right(False, second_half[:], last, HALF)
+        late_fetched = held.tile([P, last - 1, V - EARLY], F32, name="late_fetched", tag="fetched1", align_bytes=64)
+        late_right = [late_first[:]] + [late_fetched[:, t - 1, :] for t in range(1, last)]
+        for t in range(1, last):
+            fetch_right(False, late_right[t], t, EARLY)
         subtract(early_diff[:, last, 0:HALF], last, 0, first_half[:])
         subtract(early_diff[:, last, HALF:EARLY], last, HALF, second_half[:, 0 : EARLY - HALF])
+        w2_codes = held.tile([P, N], U32, name="w2_codes", tag="fetched2", align_bytes=64)
+        nc.vector.quantize_mx(out=w2_codes[:].bitcast(FP8X4), scales=w2_scales[:], in_=w2_bf[:].rearrange("p n j -> p (n j)"))
         late_right.append(second_half[:, EARLY - HALF : HALF])
 
         z_first = held.tile([P, HALF, PACK], BF16, name="z_first", tag="z_first_then_late", align_bytes=64)

@@ -16,8 +16,6 @@ RELU = mybir.ActivationFunctionType.Relu
 COPY = mybir.ActivationFunctionType.Copy
 SUBTRACT = mybir.AluOpType.subtract
 MAX = mybir.AluOpType.max
-MULT = mybir.AluOpType.mult
-ADD = mybir.AluOpType.add
 
 P = 128
 PACK = 4
@@ -35,7 +33,10 @@ W1_AHEAD = H // 4
 W1_LAST = H // 4
 W1_MIDDLE = H - W1_AHEAD - W1_LAST
 PLANE_0_WIDTHS = (S // 4, S // 4, S // 4, S // 8, S // 8)
-VECTOR_BANK = 2
+VECTOR_BANKS = (2,)
+PLANE_WIDTHS = (PLANE_0_WIDTHS, (S // 4,) * 4, (BANK, BANK), (BANK, BANK))
+SCALAR_COLUMNS = 3 * S
+W2_VECTOR = N // 2
 HALF = V // 2
 EARLY = 3 * V // 4
 
@@ -44,6 +45,7 @@ def tile_picked_phpair_relu_p_kernel(tc, x_words, x_scales, w1, w2, offs, left, 
     nc = tc.nc
     with ExitStack() as ctx:
         held = ctx.enter_context(tc.tile_pool(name="held", bufs=1))
+        shared = ctx.enter_context(tc.tile_pool(name="shared", bufs=1))
         psum = ctx.enter_context(tc.psum_pool(name="psum", bufs=8))
 
         offs_sb = held.tile([P, S // LIST], U16, name="offs_sb")
@@ -146,10 +148,10 @@ def tile_picked_phpair_relu_p_kernel(tc, x_words, x_scales, w1, w2, offs, left, 
             )
 
         h = []
-        last_banks = []
+        vector_banks = []
         for t in range(PACK):
             h_plane = held.tile([P, S], F32, name="h%d" % t, align_bytes=64)
-            widths = PLANE_0_WIDTHS if t == 0 else (BANK, BANK)
+            widths = PLANE_WIDTHS[t]
             for n, width in enumerate(widths):
                 c0 = sum(widths[:n])
                 bank = psum.tile([P, width], F32, name="bank")
@@ -158,10 +160,10 @@ def tile_picked_phpair_relu_p_kernel(tc, x_words, x_scales, w1, w2, offs, left, 
                     first_pass(bank[:, EARLY_PLACES - c0 : width], t, EARLY_PLACES, c0 + width - EARLY_PLACES)
                 else:
                     first_pass(bank[:], t, c0, width)
-                if t == PACK - 1:
-                    last_banks.append((c0, width, bank))
+                if t * S + c0 >= SCALAR_COLUMNS:
+                    vector_banks.append((h_plane[:, c0 : c0 + width], bank))
                 else:
-                    copy = nc.vector.tensor_copy if t == 0 and n == VECTOR_BANK else nc.scalar.copy
+                    copy = nc.vector.tensor_copy if t == 0 and n in VECTOR_BANKS else nc.scalar.copy
                     copy(h_plane[:, c0 : c0 + width], bank[:])
             h.append(h_plane)
 
@@ -199,32 +201,36 @@ def tile_picked_phpair_relu_p_kernel(tc, x_words, x_scales, w1, w2, offs, left, 
                 queue.dma_start(out_rows[:, a0:a1, v0 : v0 + width], result[:, a0:a1, :])
 
         early_diff = held.tile([P, PACK, EARLY], F32, name="early_diff", align_bytes=64)
+        late_right = []
         for t in range(PACK - 1):
-            fetched = held.tile([P, EARLY], F32, name="fetched%d" % t, align_bytes=64)
             if t == 0:
-                fetch_right(True, fetched[:], t, 0)
+                fetched = held.tile([P, EARLY], F32, name="fetched0", align_bytes=64)
                 late_first = held.tile([P, V - EARLY], F32, name="late_first", align_bytes=64)
+                fetch_right(True, fetched[:], t, 0)
                 fetch_right(True, late_first[:], t, EARLY)
+                late_right.append(late_first[:])
             else:
+                fetched = held.tile([P, EARLY], F32, name="fetched%d" % t, align_bytes=64)
                 fetch_right(False, fetched[:], t, 0)
-            subtract(early_diff[:, t, :], t, 0, fetched[:])
+            subtract(early_diff[:, t, :], t, 0, fetched[:, 0:EARLY])
             if t == 0:
-                w2_bf = held.tile([P, N, PACK], BF16, name="w2_bf", tag="fetched0", align_bytes=64)
-                nc.gpsimd.tensor_scalar(w2_bf[:], w2_raw[:].rearrange("p t n -> p n t"), 1.0, 0.0, MULT, ADD)
-                for c0, width, bank in last_banks:
-                    nc.vector.tensor_copy(h[PACK - 1][:, c0 : c0 + width], bank[:])
+                for columns, bank in vector_banks:
+                    nc.vector.tensor_copy(columns, bank[:])
+                w2_bf = held.tile([P, N, PACK], BF16, name="w2_bf", align_bytes=64)
+                nc.vector.tensor_copy(woven(w2_bf[:, 0:W2_VECTOR, :]), by_slot(w2_raw[:, :, 0:W2_VECTOR]))
         last = PACK - 1
-        first_half = held.tile([P, HALF], F32, name="first_half", tag="first_half_then_late_diff", align_bytes=64)
+        first_half = shared.tile([P, HALF], F32, name="first_half", align_bytes=64, offset=HALF * 2)
         second_half = held.tile([P, HALF], F32, name="second_half", align_bytes=64)
         fetch_right(False, first_half[:], last, 0)
         fetch_right(False, second_half[:], last, HALF)
         late_fetched = held.tile([P, last - 1, V - EARLY], F32, name="late_fetched", tag="fetched1", align_bytes=64)
-        late_right = [late_first[:]] + [late_fetched[:, t - 1, :] for t in range(1, last)]
         for t in range(1, last):
-            fetch_right(False, late_right[t], t, EARLY)
+            fetch_right(False, late_fetched[:, t - 1, :], t, EARLY)
+            late_right.append(late_fetched[:, t - 1, :])
+        nc.scalar.copy(woven(w2_bf[:, W2_VECTOR:N, :]), by_slot(w2_raw[:, :, W2_VECTOR:N]))
         subtract(early_diff[:, last, 0:HALF], last, 0, first_half[:])
         subtract(early_diff[:, last, HALF:EARLY], last, HALF, second_half[:, 0 : EARLY - HALF])
-        w2_codes = held.tile([P, N], U32, name="w2_codes", tag="fetched2", align_bytes=64)
+        w2_codes = shared.tile([P, N], U32, name="w2_codes", align_bytes=64, offset=0)
         nc.vector.quantize_mx(out=w2_codes[:].bitcast(FP8X4), scales=w2_scales[:], in_=w2_bf[:].rearrange("p n j -> p (n j)"))
         late_right.append(second_half[:, EARLY - HALF : HALF])
 
@@ -233,7 +239,7 @@ def tile_picked_phpair_relu_p_kernel(tc, x_words, x_scales, w1, w2, offs, left, 
         nc.scalar.activation(woven(z_first[:]), by_slot(early_diff[:, :, 0:HALF]), RELU)
         nc.scalar.activation(woven(z_middle[:]), by_slot(early_diff[:, :, HALF:EARLY]), RELU)
 
-        late_diff = held.tile([P, PACK, V - EARLY], F32, name="late_diff", tag="first_half_then_late_diff", align_bytes=64)
+        late_diff = shared.tile([P, PACK, V - EARLY], F32, name="late_diff", align_bytes=64, offset=N * 4)
         for t in range(PACK):
             subtract(late_diff[:, t, :], t, EARLY, late_right[t])
 

@@ -16,6 +16,8 @@ RELU = mybir.ActivationFunctionType.Relu
 COPY = mybir.ActivationFunctionType.Copy
 SUBTRACT = mybir.AluOpType.subtract
 MAX = mybir.AluOpType.max
+MULT = mybir.AluOpType.mult
+ADD = mybir.AluOpType.add
 
 P = 128
 PACK = 4
@@ -36,7 +38,6 @@ PLANE_0_WIDTHS = (S // 4, S // 4, S // 4, S // 8, S // 8)
 VECTOR_BANKS = (2,)
 PLANE_WIDTHS = (PLANE_0_WIDTHS, (S // 4,) * 4, (BANK, BANK), (BANK, BANK))
 SCALAR_COLUMNS = 3 * S
-W2_VECTOR = N // 2
 HALF = V // 2
 EARLY = 3 * V // 4
 
@@ -132,6 +133,10 @@ def tile_picked_phpair_relu_p_kernel(tc, x_words, x_scales, w1, w2, offs, left, 
         def by_slot(values):
             return values.rearrange("p t (c r) -> p c t r", r=RUN)
 
+        w2_bf = held.tile([P, N, PACK], BF16, name="w2_bf", tag="w1_rest", align_bytes=64)
+        for columns in (slice(0, P), slice(P, N)):
+            nc.gpsimd.tensor_scalar(woven(w2_bf[:, columns, :]), by_slot(w2_raw[:, :, columns]), 1.0, 0.0, MULT, ADD)
+
         w2_scales = held.tile([P, N], U8, name="w2_scales", align_bytes=64)
         row_tiles = [slice(a * P, (a + 1) * P) for a in range(N // P)]
 
@@ -216,8 +221,6 @@ def tile_picked_phpair_relu_p_kernel(tc, x_words, x_scales, w1, w2, offs, left, 
             if t == 0:
                 for columns, bank in vector_banks:
                     nc.vector.tensor_copy(columns, bank[:])
-                w2_bf = held.tile([P, N, PACK], BF16, name="w2_bf", align_bytes=64)
-                nc.vector.tensor_copy(woven(w2_bf[:, 0:W2_VECTOR, :]), by_slot(w2_raw[:, :, 0:W2_VECTOR]))
         last = PACK - 1
         first_half = shared.tile([P, HALF], F32, name="first_half", align_bytes=64, offset=HALF * 2)
         second_half = held.tile([P, HALF], F32, name="second_half", align_bytes=64)
@@ -227,7 +230,6 @@ def tile_picked_phpair_relu_p_kernel(tc, x_words, x_scales, w1, w2, offs, left, 
         for t in range(1, last):
             fetch_right(False, late_fetched[:, t - 1, :], t, EARLY)
             late_right.append(late_fetched[:, t - 1, :])
-        nc.scalar.copy(woven(w2_bf[:, W2_VECTOR:N, :]), by_slot(w2_raw[:, :, W2_VECTOR:N]))
         subtract(early_diff[:, last, 0:HALF], last, 0, first_half[:])
         subtract(early_diff[:, last, HALF:EARLY], last, HALF, second_half[:, 0 : EARLY - HALF])
         w2_codes = shared.tile([P, N], U32, name="w2_codes", align_bytes=64, offset=0)

@@ -36,8 +36,8 @@ W1_LAST = H // 4
 W1_MIDDLE = H - W1_AHEAD - W1_LAST
 PLANE_0_WIDTHS = (S // 4, S // 4, S // 4, S // 8, S // 8)
 VECTOR_BANKS = (2,)
-PLANE_WIDTHS = (PLANE_0_WIDTHS, (S // 4,) * 4, (BANK, BANK), (BANK, BANK))
-SCALAR_COLUMNS = 3 * S
+PLANE_WIDTHS = (PLANE_0_WIDTHS, (S // 4,) * 4, (BANK, 3 * S // 8, S // 8), (BANK, BANK))
+SCALAR_COLUMNS = 3 * S - S // 8
 HALF = V // 2
 EARLY = 3 * V // 4
 
@@ -133,9 +133,11 @@ def tile_picked_phpair_relu_p_kernel(tc, x_words, x_scales, w1, w2, offs, left, 
         def by_slot(values):
             return values.rearrange("p t (c r) -> p c t r", r=RUN)
 
-        w2_bf = held.tile([P, N, PACK], BF16, name="w2_bf", tag="w1_rest", align_bytes=64)
-        for columns in (slice(0, P), slice(P, N)):
-            nc.gpsimd.tensor_scalar(woven(w2_bf[:, columns, :]), by_slot(w2_raw[:, :, columns]), 1.0, 0.0, MULT, ADD)
+        def round_w2(rounded, a):
+            nc.gpsimd.tensor_scalar(woven(rounded[:]), by_slot(w2_raw[:, :, a * P : (a + 1) * P]), 1.0, 0.0, MULT, ADD)
+
+        w2_first = held.tile([P, P, PACK], BF16, name="w2_first", tag="w1_rest", align_bytes=64)
+        round_w2(w2_first, 0)
 
         w2_scales = held.tile([P, N], U8, name="w2_scales", align_bytes=64)
         row_tiles = [slice(a * P, (a + 1) * P) for a in range(N // P)]
@@ -208,17 +210,15 @@ def tile_picked_phpair_relu_p_kernel(tc, x_words, x_scales, w1, w2, offs, left, 
         early_diff = held.tile([P, PACK, EARLY], F32, name="early_diff", align_bytes=64)
         late_right = []
         for t in range(PACK - 1):
+            fetched = held.tile([P, EARLY], F32, name="fetched%d" % t, align_bytes=64)
+            pieces = ((0, HALF), (HALF, EARLY)) if t == 0 else ((0, EARLY),)
+            for v0, v1 in pieces:
+                fetch_right(t == 0, fetched[:, v0:v1], t, v0)
+            for v0, v1 in pieces:
+                subtract(early_diff[:, t, v0:v1], t, v0, fetched[:, v0:v1])
             if t == 0:
-                fetched = held.tile([P, EARLY], F32, name="fetched0", align_bytes=64)
-                late_first = held.tile([P, V - EARLY], F32, name="late_first", align_bytes=64)
-                fetch_right(True, fetched[:], t, 0)
-                fetch_right(True, late_first[:], t, EARLY)
-                late_right.append(late_first[:])
-            else:
-                fetched = held.tile([P, EARLY], F32, name="fetched%d" % t, align_bytes=64)
-                fetch_right(False, fetched[:], t, 0)
-            subtract(early_diff[:, t, :], t, 0, fetched[:, 0:EARLY])
-            if t == 0:
+                w2_second = held.tile([P, P, PACK], BF16, name="w2_second", tag="fetched0", align_bytes=64)
+                round_w2(w2_second, 1)
                 for columns, bank in vector_banks:
                     nc.vector.tensor_copy(columns, bank[:])
         last = PACK - 1
@@ -226,14 +226,17 @@ def tile_picked_phpair_relu_p_kernel(tc, x_words, x_scales, w1, w2, offs, left, 
         second_half = held.tile([P, HALF], F32, name="second_half", align_bytes=64)
         fetch_right(False, first_half[:], last, 0)
         fetch_right(False, second_half[:], last, HALF)
-        late_fetched = held.tile([P, last - 1, V - EARLY], F32, name="late_fetched", tag="fetched1", align_bytes=64)
-        for t in range(1, last):
-            fetch_right(False, late_fetched[:, t - 1, :], t, EARLY)
-            late_right.append(late_fetched[:, t - 1, :])
+        late_fetched = held.tile([P, last, V - EARLY], F32, name="late_fetched", tag="fetched1", align_bytes=64)
+        for t in range(last):
+            fetch_right(False, late_fetched[:, t, :], t, EARLY)
+            late_right.append(late_fetched[:, t, :])
         subtract(early_diff[:, last, 0:HALF], last, 0, first_half[:])
         subtract(early_diff[:, last, HALF:EARLY], last, HALF, second_half[:, 0 : EARLY - HALF])
         w2_codes = shared.tile([P, N], U32, name="w2_codes", align_bytes=64, offset=0)
-        nc.vector.quantize_mx(out=w2_codes[:].bitcast(FP8X4), scales=w2_scales[:], in_=w2_bf[:].rearrange("p n j -> p (n j)"))
+        for a, rounded in enumerate((w2_first, w2_second)):
+            nc.vector.quantize_mx(
+                out=w2_codes[:, row_tiles[a]].bitcast(FP8X4), scales=w2_scales[:, row_tiles[a]], in_=rounded[:].rearrange("p n j -> p (n j)")
+            )
         late_right.append(second_half[:, EARLY - HALF : HALF])
 
         z_first = held.tile([P, HALF, PACK], BF16, name="z_first", tag="z_first_then_late", align_bytes=64)

@@ -40,6 +40,9 @@ PLANE_WIDTHS = (PLANE_0_WIDTHS, (S // 4,) * 4, (BANK, 3 * S // 8, S // 8), (BANK
 SCALAR_COLUMNS = 3 * S - S // 8
 HALF = V // 2
 EARLY = 3 * V // 4
+PLANE_1_FETCH = 4096
+WARM_ROWS = 32
+WARM_PASSES = 4
 
 
 def tile_picked_phpair_relu_p_kernel(tc, x_words, x_scales, w1, w2, offs, left, right, out):
@@ -196,7 +199,7 @@ def tile_picked_phpair_relu_p_kernel(tc, x_words, x_scales, w1, w2, offs, left, 
                 bank = psum.tile([P, width], F32, name="bank")
                 nc.tensor.matmul_mx(
                     out=bank[:],
-                    lhsT=w2_codes[:, row_tiles[a]].bitcast(FP8X4),
+                    lhsT=w2_codes[a][:].bitcast(FP8X4),
                     lhsT_scale=w2_scales[:, row_tiles[a]],
                     rhs=z_codes[:].bitcast(FP8X4),
                     rhs_scale=z_scales[:],
@@ -210,7 +213,10 @@ def tile_picked_phpair_relu_p_kernel(tc, x_words, x_scales, w1, w2, offs, left, 
         early_diff = held.tile([P, PACK, EARLY], F32, name="early_diff", align_bytes=64)
         late_right = []
         for t in range(PACK - 1):
-            fetched = held.tile([P, EARLY], F32, name="fetched%d" % t, align_bytes=64)
+            if t == 1:
+                fetched = shared.tile([P, EARLY], F32, name="fetched1", align_bytes=64, offset=PLANE_1_FETCH)
+            else:
+                fetched = held.tile([P, EARLY], F32, name="fetched%d" % t, align_bytes=64)
             pieces = ((0, HALF), (HALF, EARLY)) if t == 0 else ((0, EARLY),)
             for v0, v1 in pieces:
                 fetch_right(t == 0, fetched[:, v0:v1], t, v0)
@@ -221,22 +227,37 @@ def tile_picked_phpair_relu_p_kernel(tc, x_words, x_scales, w1, w2, offs, left, 
                 round_w2(w2_second, 1)
                 for columns, bank in vector_banks:
                     nc.vector.tensor_copy(columns, bank[:])
+        def quantise_w2(a, rounded):
+            nc.vector.quantize_mx(
+                out=w2_codes[a][:].bitcast(FP8X4), scales=w2_scales[:, row_tiles[a]], in_=rounded[:].rearrange("p n j -> p (n j)")
+            )
+
+        w2_codes = [shared.tile([P, P], U32, name="w2_codes0", align_bytes=64, offset=PLANE_1_FETCH + 512)]
+        quantise_w2(0, w2_first)
+        warm_bank = psum.tile([WARM_ROWS, BANK], F32, name="bank")
+        for n in range(WARM_PASSES):
+            nc.tensor.matmul_mx(
+                out=warm_bank[:],
+                lhsT=w2_codes[0][:, 0:WARM_ROWS].bitcast(FP8X4),
+                lhsT_scale=w2_scales[:, 0:WARM_ROWS],
+                rhs=w1_codes[:].bitcast(FP8X4),
+                rhs_scale=w1_scales[:],
+                start=True,
+                stop=True,
+            )
         last = PACK - 1
         first_half = shared.tile([P, HALF], F32, name="first_half", align_bytes=64, offset=HALF * 2)
         second_half = held.tile([P, HALF], F32, name="second_half", align_bytes=64)
         fetch_right(False, first_half[:], last, 0)
         fetch_right(False, second_half[:], last, HALF)
-        late_fetched = held.tile([P, last, V - EARLY], F32, name="late_fetched", tag="fetched1", align_bytes=64)
+        late_fetched = shared.tile([P, last, V - EARLY], F32, name="late_fetched", align_bytes=64, offset=PLANE_1_FETCH - 1024)
         for t in range(last):
             fetch_right(False, late_fetched[:, t, :], t, EARLY)
             late_right.append(late_fetched[:, t, :])
         subtract(early_diff[:, last, 0:HALF], last, 0, first_half[:])
         subtract(early_diff[:, last, HALF:EARLY], last, HALF, second_half[:, 0 : EARLY - HALF])
-        w2_codes = shared.tile([P, N], U32, name="w2_codes", align_bytes=64, offset=0)
-        for a, rounded in enumerate((w2_first, w2_second)):
-            nc.vector.quantize_mx(
-                out=w2_codes[:, row_tiles[a]].bitcast(FP8X4), scales=w2_scales[:, row_tiles[a]], in_=rounded[:].rearrange("p n j -> p (n j)")
-            )
+        w2_codes.append(shared.tile([P, P], U32, name="w2_codes1", align_bytes=64, offset=HALF * 2))
+        quantise_w2(1, w2_second)
         late_right.append(second_half[:, EARLY - HALF : HALF])
 
         z_first = held.tile([P, HALF, PACK], BF16, name="z_first", tag="z_first_then_late", align_bytes=64)

@@ -189,25 +189,33 @@ def tile_picked_phpair_relu_p_kernel(tc, x_words, x_scales, w1, w2, offs, left, 
 
         out_rows = out.rearrange("(a p) v -> p a v", p=P)
 
-        def second_product(z_bf, v0, copies, stores):
-            width = z_bf.shape[1]
+        def quantise_z(v0, width, pieces):
             z_codes = held.tile([P, width], U32, name="z_codes%d" % v0, align_bytes=64)
             z_scales = held.tile([P, width], U8, name="z_scales%d" % v0, align_bytes=64)
-            nc.vector.quantize_mx(out=z_codes[:].bitcast(FP8X4), scales=z_scales[:], in_=z_bf[:].rearrange("p v t -> p (v t)"))
-            result = held.tile([P, N // P, width], F32, name="result%d" % v0, align_bytes=64)
-            for a, copy in enumerate(copies):
-                bank = psum.tile([P, width], F32, name="bank")
-                nc.tensor.matmul_mx(
-                    out=bank[:],
-                    lhsT=w2_codes[a][:].bitcast(FP8X4),
-                    lhsT_scale=w2_scales[:, row_tiles[a]],
-                    rhs=z_codes[:].bitcast(FP8X4),
-                    rhs_scale=z_scales[:],
-                    start=True,
-                    stop=True,
+            for c0, z_bf in pieces:
+                columns = slice(c0, c0 + z_bf.shape[1])
+                nc.vector.quantize_mx(
+                    out=z_codes[:, columns].bitcast(FP8X4), scales=z_scales[:, columns], in_=z_bf[:].rearrange("p v t -> p (v t)")
                 )
-                copy(result[:, a, :], bank[:])
-            for queue, a0, a1 in stores:
+            return z_codes[:], z_scales[:]
+
+        def second_product(z, v0, groups):
+            z_codes, z_scales = z
+            width = z_codes.shape[1]
+            result = held.tile([P, N // P, width], F32, name="result%d" % v0, align_bytes=64)
+            for a0, a1, copy, queue in groups:
+                bank = psum.tile([P, a1 - a0, width], F32, name="bank")
+                for a in range(a0, a1):
+                    nc.tensor.matmul_mx(
+                        out=bank[:, a - a0, :],
+                        lhsT=w2_codes[a][:].bitcast(FP8X4),
+                        lhsT_scale=w2_scales[:, row_tiles[a]],
+                        rhs=z_codes.bitcast(FP8X4),
+                        rhs_scale=z_scales,
+                        start=True,
+                        stop=True,
+                    )
+                copy(result[:, a0:a1, :], bank[:])
                 queue.dma_start(out_rows[:, a0:a1, v0 : v0 + width], result[:, a0:a1, :])
 
         early_diff = held.tile([P, PACK, EARLY], F32, name="early_diff", align_bytes=64)
@@ -269,8 +277,17 @@ def tile_picked_phpair_relu_p_kernel(tc, x_words, x_scales, w1, w2, offs, left, 
         for t in range(PACK):
             subtract(late_diff[:, t, :], t, EARLY, late_right[t])
 
-        second_product(z_first, 0, (nc.scalar.copy, nc.scalar.copy), ((nc.sync, 0, 1), (nc.sync, 1, 2)))
-        z_late = held.tile([P, V - EARLY, PACK], BF16, name="z_late", tag="z_first_then_late", align_bytes=64)
-        nc.vector.tensor_scalar(woven(z_late[:]), by_slot(late_diff[:]), 0.0, None, MAX)
-        second_product(z_middle, HALF, (nc.scalar.copy, nc.scalar.copy), ((nc.sync, 0, 2),))
-        second_product(z_late, EARLY, (nc.scalar.copy, nc.vector.tensor_copy), ((nc.scalar, 0, 1), (nc.sync, 1, 2)))
+        late = V - EARLY
+        cut = late // 2
+        z_scalar = held.tile([P, late - cut, PACK], BF16, name="z_scalar", align_bytes=64)
+        nc.scalar.activation(woven(z_scalar[:]), by_slot(late_diff[:, :, cut:late]), RELU)
+        first_codes, first_scales = quantise_z(0, HALF, ((0, z_first),))
+        quarter = V // 4
+        second_product((first_codes[:, 0:quarter], first_scales[:, 0:quarter]), 0, ((0, 1, nc.scalar.copy, nc.sync), (1, 2, nc.scalar.copy, nc.sync)))
+        second_product((first_codes[:, quarter:HALF], first_scales[:, quarter:HALF]), quarter, ((0, 2, nc.scalar.copy, nc.sync),))
+        z_vector = held.tile([P, cut, PACK], BF16, name="z_vector", tag="z_first_then_late", align_bytes=64)
+        nc.vector.tensor_scalar(woven(z_vector[:]), by_slot(late_diff[:, :, 0:cut]), 0.0, None, MAX)
+        second_product(quantise_z(HALF, EARLY - HALF, ((0, z_middle),)), HALF, ((0, 2, nc.scalar.copy, nc.sync),))
+        second_product(
+            quantise_z(EARLY, late, ((cut, z_scalar), (0, z_vector))), EARLY, ((0, 1, nc.scalar.copy, nc.scalar), (1, 2, nc.vector.tensor_copy, nc.sync))
+        )

@@ -41,8 +41,6 @@ SCALAR_COLUMNS = 3 * S - S // 8
 HALF = V // 2
 EARLY = 3 * V // 4
 PLANE_1_FETCH = 4096
-WARM_ROWS = 32
-WARM_PASSES = 4
 
 
 def tile_picked_phpair_relu_p_kernel(tc, x_words, x_scales, w1, w2, offs, left, right, out):
@@ -242,17 +240,6 @@ def tile_picked_phpair_relu_p_kernel(tc, x_words, x_scales, w1, w2, offs, left, 
 
         w2_codes = [shared.tile([P, P], U32, name="w2_codes0", align_bytes=64, offset=PLANE_1_FETCH + 512)]
         quantise_w2(0, w2_first)
-        warm_bank = psum.tile([WARM_ROWS, BANK], F32, name="bank")
-        for n in range(WARM_PASSES):
-            nc.tensor.matmul_mx(
-                out=warm_bank[:],
-                lhsT=w2_codes[0][:, 0:WARM_ROWS].bitcast(FP8X4),
-                lhsT_scale=w2_scales[:, 0:WARM_ROWS],
-                rhs=w1_codes[:].bitcast(FP8X4),
-                rhs_scale=w1_scales[:],
-                start=True,
-                stop=True,
-            )
         last = PACK - 1
         first_half = shared.tile([P, HALF], F32, name="first_half", align_bytes=64, offset=HALF * 2)
         second_half = held.tile([P, HALF], F32, name="second_half", align_bytes=64)

from contextlib import ExitStack

import concourse.mybir as mybir

K, T, S, H, N, V = 512, 2048, 1024, 512, 256, 512
FLOPS = 2 * K * H * S + 2 * H * N * V

F32 = mybir.dt.float32
BF16 = mybir.dt.bfloat16
I32 = mybir.dt.int32
U32 = mybir.dt.uint32
U16 = mybir.dt.uint16
U8 = mybir.dt.uint8
FP8X4 = mybir.dt.float8_e4m3fn_x4
RELU = mybir.ActivationFunctionType.Relu
COPY = mybir.ActivationFunctionType.Copy
SUBTRACT = mybir.AluOpType.subtract
MAX = mybir.AluOpType.max
MULT = mybir.AluOpType.mult
ADD = mybir.AluOpType.add

P = 128
PACK = 4
LIST = 16
BLOCKS = K // 32
BLOCK_PARTITIONS = P // BLOCKS
QUADRANT = 32
QUADRANT_ROWS = QUADRANT // BLOCK_PARTITIONS
BANK = 512
RUN = 4

EARLY_PLACES = 3 * S // 4
LATE_PLACES = S - EARLY_PLACES
W1_AHEAD = H // 4
W1_LAST = H // 4
W1_MIDDLE = H - W1_AHEAD - W1_LAST
PLANE_0_WIDTHS = (S // 4, S // 4, S // 4, S // 8, S // 8)
VECTOR_BANKS = (2,)
PLANE_WIDTHS = (PLANE_0_WIDTHS, (S // 4,) * 4, (BANK, 3 * S // 8, S // 8), (BANK, BANK))
SCALAR_COLUMNS = 3 * S - S // 8
HALF = V // 2
EARLY = 3 * V // 4
PLANE_1_FETCH = 4096


def tile_picked_phpair_relu_p_kernel(tc, x_words, x_scales, w1, w2, offs, left, right, out):
    nc = tc.nc
    with ExitStack() as ctx:
        held = ctx.enter_context(tc.tile_pool(name="held", bufs=1))
        shared = ctx.enter_context(tc.tile_pool(name="shared", bufs=1))
        psum = ctx.enter_context(tc.psum_pool(name="psum", bufs=8))

        offs_sb = held.tile([P, S // LIST], U16, name="offs_sb")
        left_sb = held.tile([P, V // LIST], U16, name="left_sb")
        right_sb = held.tile([P, V // LIST], U16, name="right_sb")
        scale_table = held.tile([P, T], U8, name="scale_table", align_bytes=64)
        word_table = held.tile([P, T], U32, name="word_table", align_bytes=64)
        w1_rows = w1.rearrange("(p j) c -> p j c", j=PACK)
        w1_ahead = held.tile([P, PACK, W1_AHEAD], F32, name="w1_ahead", align_bytes=64)
        w1_behind = held.tile([P, PACK, H - W1_AHEAD], F32, name="w1_behind", align_bytes=64)

        nc.vector.memset(scale_table[:].bitcast(I32), 0)
        nc.sync.dma_start(w1_ahead[:], w1_rows[:, :, 0:W1_AHEAD])
        nc.sync.dma_start(offs_sb[:], offs)
        nc.sync.dma_start(scale_table[0:P:BLOCK_PARTITIONS, :].bitcast(I32), x_scales[0].bitcast(I32))
        nc.sync.dma_start(word_table[:].bitcast(I32), x_words[0].rearrange("p n t -> p (n t)").bitcast(I32))
        nc.sync.dma_start(w1_behind[:, :, 0:W1_MIDDLE], w1_rows[:, :, W1_AHEAD : H - W1_LAST])
        nc.sync.dma_start(w1_behind[:, :, W1_MIDDLE:], w1_rows[:, :, H - W1_LAST : H])

        nc.sync.dma_start(right_sb[:], right)
        nc.sync.dma_start(left_sb[:], left)

        def entries(list_sb, v0, count):
            return list_sb[:, v0 // LIST : (v0 + count) // LIST]

        x_scale_rows = held.tile([P, S], U8, name="x_scale_rows", align_bytes=64)
        nc.vector.memset(x_scale_rows[:].bitcast(I32), 0)
        picked_scales = held.tile([P, S], U8, name="picked_scales", align_bytes=64)
        nc.vector.tensor_copy(picked_scales[:], scale_table[:].indirect(offs_sb[:]))
        for r in range(QUADRANT_ROWS):
            nc.sync.dma_start(
                x_scale_rows[r:P:QUADRANT, :].bitcast(I32),
                picked_scales[BLOCK_PARTITIONS * r : P : QUADRANT, :].bitcast(I32),
            )

        early_codes = held.tile([P, EARLY_PLACES], U32, name="early_codes", align_bytes=64)
        nc.vector.tensor_copy(early_codes[:], word_table[:].indirect(entries(offs_sb, 0, EARLY_PLACES)))

        w1_first = held.tile([P, 1, P, PACK], BF16, name="w1_first", tag="reused", align_bytes=64)
        w1_rest = held.tile([P, PACK - 1, P, PACK], BF16, name="w1_rest", align_bytes=64)

        def w1_bf(t0, t1):
            return w1_first[:] if t0 == 0 else w1_rest[:, t0 - 1 : t1 - 1]

        def round_w1(raw, c0, t0, t1):
            c1 = c0 + raw.shape[2]
            nc.scalar.copy(
                w1_bf(t0, t1)[:, :, c0 // PACK : c1 // PACK, :].rearrange("p t (g s) j -> p t g j s", s=RUN),
                raw.rearrange("p j (g t s) -> p t g j s", t=PACK, s=RUN)[:, t0:t1],
            )

        round_w1(w1_ahead[:], 0, 0, 1)
        round_w1(w1_ahead[:], 0, 1, PACK)
        for t in (0, 1):
            round_w1(w1_behind[:, :, 0:W1_MIDDLE], W1_AHEAD, t, t + 1)
        for t in (0, 1):
            round_w1(w1_behind[:, :, W1_MIDDLE:], H - W1_LAST, t, t + 1)
        round_w1(w1_behind[:], W1_AHEAD, 2, PACK)

        w2_raw = held.tile([P, PACK, N], F32, name="w2_raw", tag="scale_table", align_bytes=64)
        w2_rows = w2.rearrange("(g t s) n -> t g s n", t=PACK, s=RUN)
        for t in range(PACK):
            nc.sync.dma_start(w2_raw[:, t, :], w2_rows[t])

        w1_codes = held.tile([P, H], U32, name="w1_codes", align_bytes=64)
        w1_scales = held.tile([P, H], U8, name="w1_scales", align_bytes=64)

        def quantise_w1(t0, t1):
            nc.vector.quantize_mx(
                out=w1_codes[:, t0 * P : t1 * P].bitcast(FP8X4),
                scales=w1_scales[:, t0 * P : t1 * P],
                in_=w1_bf(t0, t1).rearrange("p t m j -> p (t m j)"),
            )

        quantise_w1(0, 1)
        quantise_w1(1, 2)
        late_codes = held.tile([P, LATE_PLACES], U32, name="late_codes", tag="reused", align_bytes=64)
        nc.vector.tensor_copy(late_codes[:], word_table[:].indirect(entries(offs_sb, EARLY_PLACES, LATE_PLACES)))
        quantise_w1(2, PACK)

        def woven(values):
            return values.rearrange("p (c r) t -> p c t r", r=RUN)

        def by_slot(values):
            return values.rearrange("p t (c r) -> p c t r", r=RUN)

        def round_w2(rounded, a):
            nc.gpsimd.tensor_scalar(woven(rounded[:]), by_slot(w2_raw[:, :, a * P : (a + 1) * P]), 1.0, 0.0, MULT, ADD)

        w2_first = held.tile([P, P, PACK], BF16, name="w2_first", tag="w1_rest", align_bytes=64)
        round_w2(w2_first, 0)

        w2_scales = held.tile([P, N], U8, name="w2_scales", align_bytes=64)
        row_tiles = [slice(a * P, (a + 1) * P) for a in range(N // P)]

        def first_pass(bank, t, c0, width):
            codes, x0 = (early_codes, c0) if c0 < EARLY_PLACES else (late_codes, c0 - EARLY_PLACES)
            nc.tensor.matmul_mx(
                out=bank,
                lhsT=w1_codes[:, t * P : (t + 1) * P].bitcast(FP8X4),
                lhsT_scale=w1_scales[:, t * P : (t + 1) * P],
                rhs=codes[:, x0 : x0 + width].bitcast(FP8X4),
                rhs_scale=x_scale_rows[:, c0 : c0 + width],
                start=True,
                stop=True,
            )

        h = []
        vector_banks = []
        for t in range(PACK):
            h_plane = held.tile([P, S], F32, name="h%d" % t, align_bytes=64)
            widths = PLANE_WIDTHS[t]
            for n, width in enumerate(widths):
                c0 = sum(widths[:n])
                bank = psum.tile([P, width], F32, name="bank")
                if c0 < EARLY_PLACES < c0 + width:
                    first_pass(bank[:, 0 : EARLY_PLACES - c0], t, c0, EARLY_PLACES - c0)
                    first_pass(bank[:, EARLY_PLACES - c0 : width], t, EARLY_PLACES, c0 + width - EARLY_PLACES)
                else:
                    first_pass(bank[:], t, c0, width)
                if t * S + c0 >= SCALAR_COLUMNS:
                    vector_banks.append((h_plane[:, c0 : c0 + width], bank))
                else:
                    copy = nc.vector.tensor_copy if t == 0 and n in VECTOR_BANKS else nc.scalar.copy
                    copy(h_plane[:, c0 : c0 + width], bank[:])
            h.append(h_plane)

        def fetch_right(on_vector, fetched, t, v0):
            window = h[t][:].indirect(entries(right_sb, v0, fetched.shape[1]))
            if on_vector:
                nc.vector.tensor_copy(fetched, window)
            else:
                nc.scalar.activation(fetched, window, COPY)

        def subtract(diff, t, v0, fetched):
            nc.vector.tensor_tensor(diff, h[t][:].indirect(entries(left_sb, v0, fetched.shape[1])), fetched, SUBTRACT)

        out_rows = out.rearrange("(a p) v -> p a v", p=P)

        def quantise_z(v0, width, pieces):
            z_codes = held.tile([P, width], U32, name="z_codes%d" % v0, align_bytes=64)
            z_scales = held.tile([P, width], U8, name="z_scales%d" % v0, align_bytes=64)
            for c0, z_bf in pieces:
                columns = slice(c0, c0 + z_bf.shape[1])
                nc.vector.quantize_mx(
                    out=z_codes[:, columns].bitcast(FP8X4), scales=z_scales[:, columns], in_=z_bf[:].rearrange("p v t -> p (v t)")
                )
            return z_codes[:], z_scales[:]

        def second_product(z, v0, groups):
            z_codes, z_scales = z
            width = z_codes.shape[1]
            result = held.tile([P, N // P, width], F32, name="result%d" % v0, align_bytes=64)
            for a0, a1, copy, queue in groups:
                bank = psum.tile([P, a1 - a0, width], F32, name="bank")
                for a in range(a0, a1):
                    nc.tensor.matmul_mx(
                        out=bank[:, a - a0, :],
                        lhsT=w2_codes[a][:].bitcast(FP8X4),
                        lhsT_scale=w2_scales[:, row_tiles[a]],
                        rhs=z_codes.bitcast(FP8X4),
                        rhs_scale=z_scales,
                        start=True,
                        stop=True,
                    )
                copy(result[:, a0:a1, :], bank[:])
                queue.dma_start(out_rows[:, a0:a1, v0 : v0 + width], result[:, a0:a1, :])

        early_diff = held.tile([P, PACK, EARLY], F32, name="early_diff", align_bytes=64)
        late_right = []
        for t in range(PACK - 1):
            if t == 1:
                fetched = shared.tile([P, EARLY], F32, name="fetched1", align_bytes=64, offset=PLANE_1_FETCH)
            else:
                fetched = held.tile([P, EARLY], F32, name="fetched%d" % t, align_bytes=64)
            pieces = ((0, HALF), (HALF, EARLY)) if t == 0 else ((0, EARLY),)
            for v0, v1 in pieces:
                fetch_right(t == 0, fetched[:, v0:v1], t, v0)
            for v0, v1 in pieces:
                subtract(early_diff[:, t, v0:v1], t, v0, fetched[:, v0:v1])
            if t == 0:
                w2_second = held.tile([P, P, PACK], BF16, name="w2_second", tag="fetched0", align_bytes=64)
                round_w2(w2_second, 1)
                for columns, bank in vector_banks:
                    nc.vector.tensor_copy(columns, bank[:])
        def quantise_w2(a, rounded):
            nc.vector.quantize_mx(
                out=w2_codes[a][:].bitcast(FP8X4), scales=w2_scales[:, row_tiles[a]], in_=rounded[:].rearrange("p n j -> p (n j)")
            )

        w2_codes = [shared.tile([P, P], U32, name="w2_codes0", align_bytes=64, offset=PLANE_1_FETCH + 512)]
        quantise_w2(0, w2_first)
        last = PACK - 1
        first_half = shared.tile([P, HALF], F32, name="first_half", align_bytes=64, offset=HALF * 2)
        second_half = held.tile([P, HALF], F32, name="second_half", align_bytes=64)
        fetch_right(False, first_half[:], last, 0)
        fetch_right(False, second_half[:], last, HALF)
        late_fetched = shared.tile([P, last, V - EARLY], F32, name="late_fetched", align_bytes=64, offset=PLANE_1_FETCH - 1024)
        for t in range(last):
            fetch_right(False, late_fetched[:, t, :], t, EARLY)
            late_right.append(late_fetched[:, t, :])
        subtract(early_diff[:, last, 0:HALF], last, 0, first_half[:])
        subtract(early_diff[:, last, HALF:EARLY], last, HALF, second_half[:, 0 : EARLY - HALF])
        w2_codes.append(shared.tile([P, P], U32, name="w2_codes1", align_bytes=64, offset=HALF * 2))
        quantise_w2(1, w2_second)
        late_right.append(second_half[:, EARLY - HALF : HALF])

        z_first = held.tile([P, HALF, PACK], BF16, name="z_first", tag="z_first_then_late", align_bytes=64)
        z_middle = held.tile([P, EARLY - HALF, PACK], BF16, name="z_middle", align_bytes=64)
        nc.scalar.activation(woven(z_first[:]), by_slot(early_diff[:, :, 0:HALF]), RELU)
        nc.scalar.activation(woven(z_middle[:]), by_slot(early_diff[:, :, HALF:EARLY]), RELU)

        late_diff = shared.tile([P, PACK, V - EARLY], F32, name="late_diff", align_bytes=64, offset=N * 4)
        for t in range(PACK):
            subtract(late_diff[:, t, :], t, EARLY, late_right[t])

        late = V - EARLY
        cut = late // 2
        z_scalar = held.tile([P, late - cut, PACK], BF16, name="z_scalar", align_bytes=64)
        nc.scalar.activation(woven(z_scalar[:]), by_slot(late_diff[:, :, cut:late]), RELU)
        first_codes, first_scales = quantise_z(0, HALF, ((0, z_first),))
        quarter = V // 4
        second_product((first_codes[:, 0:quarter], first_scales[:, 0:quarter]), 0, ((0, 1, nc.scalar.copy, nc.sync), (1, 2, nc.scalar.copy, nc.sync)))
        second_product((first_codes[:, quarter:HALF], first_scales[:, quarter:HALF]), quarter, ((0, 2, nc.scalar.copy, nc.sync),))
        z_vector = held.tile([P, cut, PACK], BF16, name="z_vector", tag="z_first_then_late", align_bytes=64)
        nc.vector.tensor_scalar(woven(z_vector[:]), by_slot(late_diff[:, :, 0:cut]), 0.0, None, MAX)
        second_product(quantise_z(HALF, EARLY - HALF, ((0, z_middle),)), HALF, ((0, 2, nc.scalar.copy, nc.sync),))
        second_product(
            quantise_z(EARLY, late, ((cut, z_scalar), (0, z_vector))), EARLY, ((0, 1, nc.scalar.copy, nc.scalar), (1, 2, nc.vector.tensor_copy, nc.sync))
        )
